import numpy as np
import ml_dtypes


def mxq(x, axis, fmt="e4m3"):
    dtype, down = {"e4m3": (ml_dtypes.float8_e4m3fn, 7), "e5m2": (ml_dtypes.float8_e5m2, 14)}[fmt]
    v = np.moveaxis(np.asarray(x, np.float32).astype(ml_dtypes.bfloat16).astype(np.float64), axis, -1)
    blocks = v.reshape(v.shape[:-1] + (-1, 32))
    amax = np.abs(blocks).max(-1, keepdims=True)
    byte = np.maximum(np.where(amax > 0, np.frexp(amax)[1] - 1 + 127, 0) - down, 1)
    scale = np.exp2(byte - 127.0)
    codes = (blocks / scale).astype(np.float32).astype(dtype).astype(np.float64)
    return np.moveaxis((codes * scale).reshape(v.shape), -1, axis)


WIDE = False


def mx_kscale(k):
    if not WIDE:
        return np.ones(k)
    levels = np.array([10, -10, 5, -5, 0])
    if k % 512:
        return np.exp2(np.random.permutation(np.resize(levels, k // 32))).repeat(32)
    a = np.empty((k // 512, 16))
    for p in range(k // 512):
        a[p, :8] = np.random.permutation(np.resize(levels, 8))
        for g in range(8):
            far = levels[np.abs(levels - a[p, g]) >= 10]
            a[p, g + 8] = far[np.random.randint(len(far))]
    return np.exp2(a.ravel()).repeat(32)


BF16 = ml_dtypes.bfloat16


def bf(x):
    return np.asarray(x, np.float32).astype(BF16)


def f64(x):
    return np.asarray(x).astype(np.float64)


E2M1 = np.array([0.0, 0.5, 1.0, 1.5, 2.0, 3.0, 4.0, 6.0, -0.0, -0.5, -1.0, -1.5, -2.0, -3.0, -4.0, -6.0])


def pack_weight(w, fmt):
    k, n = w.shape
    w = f64(bf(w)).reshape(k // 32, 32, n)
    amax = np.abs(w).max(1)
    if fmt == "e4m3":
        byte = np.frexp(amax)[1] - 1 + 127 - 7
    else:
        mant, ex = np.frexp(amax / 6.0)
        byte = np.where(mant > 0.5, ex, ex - 1) + 127
    byte = np.clip(np.where(amax > 0, byte, 1), 1, 254)
    scaled = (w * np.exp2(127.0 - byte)[:, None, :]).reshape(k, n).astype(np.float32)
    by_word = np.ascontiguousarray(scaled.reshape(k // 512, 128, 4, n).transpose(0, 1, 3, 2))
    if fmt == "e4m3":
        words = by_word.astype(ml_dtypes.float8_e4m3fn).view(np.uint8)
    else:
        c = by_word.astype(ml_dtypes.float4_e2m1fn).view(np.uint8) & 0xF
        words = c[..., 0::2] | (c[..., 1::2] << 4)
    return np.ascontiguousarray(words), np.ascontiguousarray(byte.astype(np.uint8).reshape(k // 512, 16, n))


def unpack_weight(words, scales, fmt):
    g, p, n, _ = words.shape
    if fmt == "e4m3":
        vals = np.ascontiguousarray(words).view(ml_dtypes.float8_e4m3fn).astype(np.float64)
    else:
        nib = np.empty((g, p, n, 4), np.uint8)
        nib[..., 0::2] = words & 0xF
        nib[..., 1::2] = words >> 4
        vals = E2M1[nib]
    vals = vals * np.repeat(np.exp2(scales.astype(np.float64) - 127.0), 8, axis=1)[..., None]
    return vals.transpose(0, 1, 3, 2).reshape(g * 512, n)

def planes(Y):
    n, m = Y.shape
    b = f64(bf(Y)).reshape(n // 32, 32, m)
    amax = np.abs(b).max(1)
    byte = np.clip(np.where(amax > 0, np.frexp(amax)[1] - 1 + 127 - 7, 1), 1, 254)
    codes = (b * np.exp2(127.0 - byte)[:, None, :]).reshape(n, m).astype(np.float32).astype(ml_dtypes.float8_e4m3fn).view(np.uint8)
    words = codes.reshape(n // 512, 128, 4, m).transpose(0, 1, 3, 2)
    return np.ascontiguousarray(words), np.ascontiguousarray(byte.astype(np.uint8).reshape(n // 512, 16, m))


NE, NV, NF, C, F = 1536, 1024, 1024, 512, 512


def setup_inputs():
    s0, s2 = mx_kscale(C), mx_kscale(C)
    t0, t2 = mx_kscale(NV), mx_kscale(NF)
    x0 = bf(np.random.standard_normal((NV, C)) * s0[None, :] * t0[:, None])
    x1 = bf(np.random.standard_normal((NE, F)))
    x2 = bf(np.random.standard_normal((NF, C)) * s2[None, :] * t2[:, None])
    inc_down = bf(np.random.standard_normal((NE, NV)) / np.sqrt(NV) / t0[None, :])
    inc_up = bf(np.random.standard_normal((NE, NF)) / np.sqrt(NF) / t2[None, :])
    w0_words, w0_scales = pack_weight(np.random.standard_normal((C, F)) / np.sqrt(C) / s0[:, None], "e4m3")
    w2_words, w2_scales = pack_weight(np.random.standard_normal((C, F)) / np.sqrt(C) / s2[:, None], "e4m3")
    return {
        "x0": x0,
        "x1": x1,
        "x2": x2,
        "inc_down": inc_down,
        "inc_up": inc_up,
        "w0_words": w0_words,
        "w0_scales": w0_scales,
        "w2_words": w2_words,
        "w2_scales": w2_scales,
    }


def incidence_message(incidence, cells, weight_words, weight_scales):
    h = mxq(f64(cells), 1, "e4m3") @ unpack_weight(weight_words, weight_scales, "e4m3")
    return mxq(f64(incidence), 1, "e4m3") @ mxq(h, 0, "e4m3")


def core(x0, x1, x2, inc_down, inc_up, w0_words, w0_scales, w2_words, w2_scales):
    m_down = incidence_message(inc_down, x0, w0_words, w0_scales)
    m_up = incidence_message(inc_up, x2, w2_words, w2_scales)
    z = f64(x1) + m_down + m_up
    return z * (1.0 / (1.0 + np.exp(-z)))


def reference(x0, x1, x2, inc_down, inc_up, w0_words, w0_scales, w2_words, w2_scales):
    R_out = core(x0, x1, x2, inc_down, inc_up, w0_words, w0_scales, w2_words, w2_scales)
    words, scales = planes(R_out)
    return R_out, words, scales

@@ -1,0 +1,308 @@
+from contextlib import ExitStack
+
+import concourse.mybir as mybir
+from concourse.masks import make_identity
+
+F32 = mybir.dt.float32
+BF16 = mybir.dt.bfloat16
+U32 = mybir.dt.uint32
+I32 = mybir.dt.int32
+U8 = mybir.dt.uint8
+FP8X4 = mybir.dt.float8_e4m3fn_x4
+ACT = mybir.ActivationFunctionType
+ALU = mybir.AluOpType
+
+NE, NV, C, F = 1536, 1024, 512, 512
+FLOPS = 2 * (2 * NV * C * F) + 2 * (2 * NE * NV * F)
+
+P = 128
+
+
+def tile_simplicialboundarycoboundarymessage_x2_kernel(
+    tc, x0, x1, x2, inc_down, inc_up, w0_words, w0_scales, w2_words, w2_scales, out_0, out_1, out_2
+):
+    nc = tc.nc
+    cells = [x0, x2]
+    incs = [inc_down, inc_up]
+    wwords = [w0_words, w2_words]
+    wscales = [w0_scales, w2_scales]
+
+    with ExitStack() as ctx:
+        keep = ctx.enter_context(tc.tile_pool(name="keep", bufs=1))
+        psum = ctx.enter_context(tc.psum_pool(name="psum", bufs=1))
+
+        def sb(name, shape, dtype):
+            return keep.tile(shape, dtype, name=name, tag=name, align_bytes=256)
+
+        grp_pool = ctx.enter_context(tc.tile_pool(name="grp_pool", bufs=8))
+
+        def grp_tile(name):
+            return grp_pool.tile([P, 512, 4], BF16, name=name, tag="grp", align_bytes=256)
+
+        def bank(b, name, shape):
+            return psum.tile(shape, F32, name=name, tag="bank%d" % b)
+
+        warm = sb("warm", [P, 1], F32)
+        nc.vector.memset(warm[:], 0.0)
+        ident = sb("ident", [P, P], F32)
+        make_identity(nc, ident[:])
+        w_codes = []
+        w_sc = []
+        for m in range(2):
+            w_codes.append(sb("w_codes%d" % m, [P, F], U32))
+            plane = sb("w_sc%d" % m, [P, F], U8)
+            nc.vector.memset(plane[:].bitcast(I32), 0)
+            w_sc.append(plane)
+        nc.scalar.activation(out=warm[:], in_=warm[:], func=ACT.Silu)
+
+        x_raw = {}
+        for m in range(2):
+            for g in range(2):
+                raw = sb("x_raw%d%d" % (m, g), [P, 4, C], BF16)
+                x_raw[m, g] = raw
+                src = cells[m][512 * g : 512 * g + 512, :].rearrange("(p t) c -> p t c", t=4)
+                if m == 0 and g == 0:
+                    nc.sync.dma_start(out=raw[:, 0:2, :], in_=src[:, 0:2, :])
+                    nc.sync.dma_start(out=raw[:, 2:4, :], in_=src[:, 2:4, :])
+                else:
+                    nc.sync.dma_start(out=raw[:], in_=src)
+                if g == 0:
+                    for q in range(4):
+                        nc.sync.dma_start(
+                            out=w_sc[m][32 * q : 32 * q + 4, :].bitcast(I32),
+                            in_=wscales[m][0, 4 * q : 4 * q + 4, :].bitcast(I32),
+                        )
+            nc.sync.dma_start(out=w_codes[m][:].bitcast(I32), in_=wwords[m][0].rearrange("p n t -> p (n t)").bitcast(I32))
+        inc_raw = {}
+        x1_raw = {}
+        for G in range(3):
+            for m in range(2):
+                raw = sb("inc_raw%d%d" % (m, G), [P, 4, NV], BF16)
+                inc_raw[m, G] = raw
+                src = incs[m][512 * G : 512 * G + 512, :].rearrange("(p t) k -> p t k", t=4)
+                if G == 0:
+                    nc.sync.dma_start(out=raw[:, 0:2, :], in_=src[:, 0:2, :])
+                    nc.sync.dma_start(out=raw[:, 2:4, :], in_=src[:, 2:4, :])
+                else:
+                    nc.sync.dma_start(out=raw[:], in_=src)
+            t1 = sb("x1_raw%d" % G, [P, 4, F], BF16)
+            x1_raw[G] = t1
+            nc.sync.dma_start(out=t1[:], in_=x1[512 * G : 512 * G + 512, :].rearrange("(p t) f -> p t f", t=4))
+
+        def scopy(out, in_):
+            nc.scalar.copy(out=out, in_=in_)
+
+        def vcopy(out, in_):
+            nc.vector.tensor_copy(out=out, in_=in_)
+
+        def quant(codes, sc, grp):
+            nc.vector.quantize_mx(
+                out=codes.bitcast(FP8X4), scales=sc, in_=grp.rearrange("p r j -> p (r j)")
+            )
+
+        def transposes(b, name, raw, k0, tp):
+            words = raw[:].rearrange("p t k -> p (t k)").bitcast(F32)
+            width = raw.shape[2] // 2
+            pt = bank(b, name, [P, 4, P])
+            for tt in range(2):
+                for u in range(2):
+                    w0 = (2 * tp + tt) * width + k0 // 2 + u
+                    nc.tensor.transpose(pt[:, 2 * tt + u, :], words[:, w0 : w0 + 255 : 2], ident[:])
+            return pt
+
+        def copy_words(copy, grp, pt, tp):
+            dst = grp[:].rearrange("p r j -> p (r j)").bitcast(F32)[:, 512 * tp : 512 * tp + 512]
+            copy(
+                dst.rearrange("p (a r u) -> p a r u", a=2, u=2),
+                pt[:].rearrange("p (a u) r -> p a r u", u=2),
+            )
+
+        x_units = [(0, 0), (0, 1), (1, 0), (1, 1)]
+        X = {}
+        x_tbanks = [(0, 1), (2, 3), (0, 1), (6, 7)]
+        s_banks = [(4, 5, 6, 7), (2, 3, 4, 5), (0, 1, 2, 3), (0, 1, 2, 3)]
+
+        def tx(i):
+            m, g = x_units[i]
+            X[i] = [transposes(x_tbanks[i][tp], "xt%d%d" % (i, tp), x_raw[m, g], 0, tp) for tp in range(2)]
+
+        x_grp, x_codes, x_sc = {}, {}, {}
+        h_ps, h_grp, h_codes, h_sc = {}, {}, {}, {}
+
+        def cx(i):
+            x_grp[i] = grp_tile("x_grp%d" % i)
+            copy_words(scopy, x_grp[i], X[i][0], 0)
+            copy_words(vcopy, x_grp[i], X[i][1], 1)
+
+        def qx(i):
+            x_codes[i] = sb("x_codes%d" % i, [P, 512], U32)
+            x_sc[i] = sb("x_sc%d" % i, [P, 512], U8)
+            quant(x_codes[i][:], x_sc[i][:], x_grp[i][:])
+
+        def s1(i):
+            m, g = x_units[i]
+            h_ps[i] = []
+            for j in range(4):
+                hp = bank(s_banks[i][j], "hp%d%d" % (i, j), [P, 4, P])
+                cols = slice(128 * j, 128 * j + 128)
+                for t in range(4):
+                    rows = slice(128 * t, 128 * t + 128)
+                    nc.tensor.matmul_mx(
+                        out=hp[:, t, :],
+                        lhsT=x_codes[i][:, rows].bitcast(FP8X4),
+                        lhsT_scale=x_sc[i][:, rows],
+                        rhs=w_codes[m][:, cols].bitcast(FP8X4),
+                        rhs_scale=w_sc[m][:, cols],
+                        start=True,
+                        stop=True,
+                    )
+                h_ps[i].append(hp)
+
+        def ch(i):
+            h_grp[i] = grp_tile("h_grp%d" % i)
+            for j in range(4):
+                copy = vcopy if j == 1 else scopy
+                copy(h_grp[i][:, 128 * j : 128 * j + 128, :], h_ps[i][j][:].rearrange("p t n -> p n t"))
+
+        def qh(i):
+            h_codes[i] = sb("h_codes%d" % i, [P, 512], U32)
+            h_sc[i] = sb("h_sc%d" % i, [P, 512], U8)
+            quant(h_codes[i][:], h_sc[i][:], h_grp[i][:])
+
+        D, d_grp, d_codes, d_sc = {}, {}, {}, {}
+
+        def td(k):
+            G, m = divmod(k, 2)
+            D[k] = {}
+            for g in range(2):
+                for tp in range(2):
+                    D[k][g, tp] = transposes(4 + 2 * g + tp, "dt%d%d%d" % (k, g, tp), inc_raw[m, G], 512 * g, tp)
+
+        def cd(k, v_share):
+            n = 0
+            for g in range(2):
+                d_grp[k, g] = grp_tile("d_grp%d%d" % (k, g))
+                for tp in range(2):
+                    copy_words(vcopy if n in v_share else scopy, d_grp[k, g], D[k][g, tp], tp)
+                    n += 1
+
+        def qd(k):
+            for g in range(2):
+                d_codes[k, g] = sb("d_codes%d%d" % (k, g), [P, 512], U32)
+                d_sc[k, g] = sb("d_sc%d%d" % (k, g), [P, 512], U8)
+                quant(d_codes[k, g][:], d_sc[k, g][:], d_grp[k, g][:])
+
+        acc = {}
+
+        def mm(k, parts):
+            G, m = divmod(k, 2)
+            width = F // parts
+            for h in range(parts):
+                cols = slice(width * h, width * h + width)
+                for t in range(4):
+                    rows = slice(128 * t, 128 * t + 128)
+                    if m == 0:
+                        acc[G, h, t] = bank(4 * h + t, "acc%d%d%d" % (G, h, t), [P, width])
+                    for g in range(2):
+                        nc.tensor.matmul_mx(
+                            out=acc[G, h, t][:],
+                            lhsT=d_codes[k, g][:, rows].bitcast(FP8X4),
+                            lhsT_scale=d_sc[k, g][:, rows],
+                            rhs=h_codes[2 * m + g][:, cols].bitcast(FP8X4),
+                            rhs_scale=h_sc[2 * m + g][:, cols],
+                            start=(m == 0 and g == 0),
+                            stop=(m == 1 and g == 1),
+                        )
+
+        z_t, r_t, o_grp, o_codes, o_sc = {}, {}, {}, {}, {}
+
+        def adds(G, h, parts):
+            width = F // parts
+            cols = slice(width * h, width * h + width)
+            if h == 0:
+                z_t[G] = keep.tile([P, 4, F], F32, name="z%d" % G, tag="z", bufs=2, align_bytes=256)
+                r_t[G] = sb("r%d" % G, [P, 4, F], F32)
+            for t in range(4):
+                nc.vector.tensor_tensor(
+                    out=z_t[G][:, t, cols], in0=acc[G, h, t][:], in1=x1_raw[G][:, t, cols], op=ALU.add
+                )
+                nc.scalar.activation(out=r_t[G][:, t, cols], in_=z_t[G][:, t, cols], func=ACT.Silu)
+
+        def finish(G, h, parts):
+            width = F // parts
+            cols = slice(width * h, width * h + width)
+            if h == 0:
+                o_grp[G] = grp_tile("o_grp%d" % G)
+                o_codes[G] = sb("o_codes%d" % G, [P, F], U32)
+                o_sc[G] = sb("o_sc%d" % G, [P, F], U8)
+            nc.vector.tensor_copy(out=o_grp[G][:, cols, :], in_=r_t[G][:, :, cols].rearrange("p t f -> p f t"))
+            nc.sync.dma_start(
+                out=out_0[512 * G : 512 * G + 512, cols].rearrange("(p t) f -> p t f", t=4), in_=r_t[G][:, :, cols]
+            )
+            quant(o_codes[G][:, cols], o_sc[G][:, cols], o_grp[G][:, cols, :])
+            nc.sync.dma_start(
+                out=out_1[G].rearrange("p m t -> p (m t)").bitcast(I32)[:, cols], in_=o_codes[G][:, cols].bitcast(I32)
+            )
+            for q in range(4):
+                nc.sync.dma_start(
+                    out=out_2[G, 4 * q : 4 * q + 4, cols].bitcast(I32),
+                    in_=o_sc[G][32 * q : 32 * q + 4, cols].bitcast(I32),
+                )
+
+        with tc.manual_schedule():
+            tx(0)
+            tx(1)
+            cx(0)
+            qx(0)
+            cx(1)
+            s1(0)
+            tx(2)
+            qx(1)
+            ch(0)
+            s1(1)
+            cx(2)
+            qh(0)
+            tx(3)
+            qx(2)
+            ch(1)
+            s1(2)
+            cx(3)
+            qh(1)
+            td(0)
+            qx(3)
+            ch(2)
+            s1(3)
+            cd(0, (1,))
+            qh(2)
+            td(1)
+            qd(0)
+            ch(3)
+            mm(0, 1)
+            qh(3)
+            cd(1, (1,))
+            td(2)
+            qd(1)
+            mm(1, 1)
+            cd(2, ())
+            qd(2)
+            adds(0, 0, 1)
+            td(3)
+            mm(2, 1)
+            cd(3, ())
+            qd(3)
+            finish(0, 0, 1)
+            td(4)
+            mm(3, 1)
+            cd(4, ())
+            qd(4)
+            adds(1, 0, 1)
+            td(5)
+            mm(4, 2)
+            cd(5, (1, 3))
+            qd(5)
+            finish(1, 0, 1)
+            mm(5, 2)
+            adds(2, 0, 2)
+            finish(2, 0, 2)
+            adds(2, 1, 2)
+            finish(2, 1, 2)

@@ -16,6 +16,17 @@ NE, NV, C, F = 1536, 1024, 512, 512
 FLOPS = 2 * (2 * NV * C * F) + 2 * (2 * NE * NV * F)
 
 P = 128
+REORD = {1: 'V', 2: 'V', 3: 'V', 4: 'V'}
+REORD_ENG = {}
+XREORD = ()
+SEQ = [('tx', (0,)), ('tx', (1,)), ('cx', (0,)), ('qx', (0,)), ('cx', (1,)), ('s1', (0,)), ('tx', (2,)), ('qx', (1,)), ('ch', (0,)), ('s1', (1,)), ('cx', (2,)), ('qh', (0,)), ('tx', (3,)), ('qx', (2,)), ('ch', (1,)), ('s1', (2,)), ('cx', (3,)), ('qh', (1,)), ('rd', (0,)), ('td', (0, 0)), ('td', (0, 1)), ('cd', (0, 0)), ('qd', (0, 0)), ('cd', (0, 1)), ('qd', (0, 1)), ('qx', (3,)), ('ch', (2,)), ('s1', (3,)), ('qh', (2,)), ('rd', (1,)), ('td', (1, 0)), ('td', (1, 1)), ('cd', (1, 0)), ('qd', (1, 0)), ('cd', (1, 1)), ('qd', (1, 1)), ('ch', (3,)), ('mm', (0, 0, 1, (0, 1, 2, 3))), ('qh', (3,)), ('rd', (2,)), ('td', (2, 0)), ('td', (2, 1)), ('cd', (2, 0)), ('qd', (2, 0)), ('cd', (2, 1)), ('qd', (2, 1)), ('mm', (1, 0, 1, (0, 1, 2, 3))), ('ad', (0, 0, 1, (0, 1, 2, 3))), ('rd', (3,)), ('td', (3, 0)), ('td', (3, 1)), ('cd', (3, 0)), ('qd', (3, 0)), ('cd', (3, 1)), ('qd', (3, 1)), ('mm', (2, 0, 1, (0, 1, 2, 3))), ('fi', (0, 0, 1)), ('rd', (4,)), ('td', (4, 0)), ('td', (4, 1)), ('cd', (4, 0)), ('qd', (4, 0)), ('cd', (4, 1)), ('qd', (4, 1)), ('mm', (3, 0, 1, (0, 1, 2, 3))), ('ad', (1, 0, 1, (0, 1, 2, 3))), ('rd', (5,)), ('td', (5, 0)), ('td', (5, 1)), ('cd', (5, 0)), ('qd', (5, 0)), ('cd', (5, 1)), ('qd', (5, 1)), ('mm', (4, 0, 2, (0, 1, 2, 3))), ('mm', (4, 1, 2, (0, 1, 2, 3))), ('fi', (1, 0, 1)), ('mm', (5, 0, 2, (0, 1, 2, 3))), ('ad', (2, 0, 2)), ('fi', (2, 0, 2)), ('mm', (5, 1, 2, (0, 1, 2, 3))), ('ad', (2, 1, 2)), ('fi', (2, 1, 2))]
+LASTPARTS = 2
+VC = {5: (1, 3)}
+XV = {}
+HV = {}
+ZE = {}
+XTB = [(0, 1), (2, 3), (0, 1), (6, 7)]
+X1LATE = 0
 
 
 def tile_simplicialboundarycoboundarymessage_x2_kernel(
@@ -85,9 +96,12 @@ def tile_simplicialboundarycoboundarymessage_x2_kernel(
                     nc.sync.dma_start(out=raw[:, 2:4, :], in_=src[:, 2:4, :])
                 else:
                     nc.sync.dma_start(out=raw[:], in_=src)
-            t1 = sb("x1_raw%d" % G, [P, 4, F], BF16)
-            x1_raw[G] = t1
-            nc.sync.dma_start(out=t1[:], in_=x1[512 * G : 512 * G + 512, :].rearrange("(p t) f -> p t f", t=4))
+            if X1LATE and G == 0:
+                continue
+            for G1 in ((0, 1) if X1LATE and G == 1 else (G,)):
+              t1 = sb("x1_raw%d" % G1, [P, 4, F], BF16)
+              x1_raw[G1] = t1
+              nc.sync.dma_start(out=t1[:], in_=x1[512 * G1 : 512 * G1 + 512, :].rearrange("(p t) f -> p t f", t=4))
 
         def scopy(out, in_):
             nc.scalar.copy(out=out, in_=in_)
@@ -100,15 +114,32 @@ def tile_simplicialboundarycoboundarymessage_x2_kernel(
                 out=codes.bitcast(FP8X4), scales=sc, in_=grp.rearrange("p r j -> p (r j)")
             )
 
-        def transposes(b, name, raw, k0, tp):
+        def transposes(b, name, raw, k0, tp, sorted_words=None):
             words = raw[:].rearrange("p t k -> p (t k)").bitcast(F32)
             width = raw.shape[2] // 2
             pt = bank(b, name, [P, 4, P])
             for tt in range(2):
                 for u in range(2):
-                    w0 = (2 * tp + tt) * width + k0 // 2 + u
-                    nc.tensor.transpose(pt[:, 2 * tt + u, :], words[:, w0 : w0 + 255 : 2], ident[:])
+                    t = 2 * tp + tt
+                    if sorted_words is not None:
+                        w0 = k0 // 2 + 128 * u
+                        src_w = sorted_words[:, t, w0 : w0 + 128]
+                    else:
+                        w0 = t * width + k0 // 2 + u
+                        src_w = words[:, w0 : w0 + 255 : 2]
+                    nc.tensor.transpose(pt[:, 2 * tt + u, :], src_w, ident[:])
             return pt
+
+        def reorder(name, raw, eng):
+            width = raw.shape[2] // 2
+            t = keep.tile([P, 4, width], F32, name=name, tag="sorted%d" % width, bufs=3, align_bytes=256)
+            srcw = raw[:].rearrange("p t k -> p (t k)").bitcast(F32).rearrange("p (q w u) -> p q u w", u=2, w=128)
+            dst = t[:].rearrange("p t k -> p (t k)").rearrange("p (q u w) -> p q u w", u=2, w=128)
+            nq = 4 * width // 256
+            for i in range(2):
+                qs = slice(nq // 2 * i, nq // 2 * (i + 1))
+                (vcopy if eng == "V" else scopy)(dst[:, qs], srcw[:, qs])
+            return t
 
         def copy_words(copy, grp, pt, tp):
             dst = grp[:].rearrange("p r j -> p (r j)").bitcast(F32)[:, 512 * tp : 512 * tp + 512]
@@ -119,20 +150,21 @@ def tile_simplicialboundarycoboundarymessage_x2_kernel(
 
         x_units = [(0, 0), (0, 1), (1, 0), (1, 1)]
         X = {}
-        x_tbanks = [(0, 1), (2, 3), (0, 1), (6, 7)]
+        x_tbanks = XTB
         s_banks = [(4, 5, 6, 7), (2, 3, 4, 5), (0, 1, 2, 3), (0, 1, 2, 3)]
 
         def tx(i):
             m, g = x_units[i]
-            X[i] = [transposes(x_tbanks[i][tp], "xt%d%d" % (i, tp), x_raw[m, g], 0, tp) for tp in range(2)]
+            srt = reorder("xs%d" % i, x_raw[m, g], XREORD[i]) if i in XREORD else None
+            X[i] = [transposes(x_tbanks[i][tp], "xt%d%d" % (i, tp), x_raw[m, g], 0, tp, srt) for tp in range(2)]
 
         x_grp, x_codes, x_sc = {}, {}, {}
         h_ps, h_grp, h_codes, h_sc = {}, {}, {}, {}
 
         def cx(i):
             x_grp[i] = grp_tile("x_grp%d" % i)
-            copy_words(scopy, x_grp[i], X[i][0], 0)
-            copy_words(vcopy, x_grp[i], X[i][1], 1)
+            for tp in range(2):
+                copy_words(vcopy if tp in XV.get(i, (1,)) else scopy, x_grp[i], X[i][tp], tp)
 
         def qx(i):
             x_codes[i] = sb("x_codes%d" % i, [P, 512], U32)
@@ -161,7 +193,7 @@ def tile_simplicialboundarycoboundarymessage_x2_kernel(
         def ch(i):
             h_grp[i] = grp_tile("h_grp%d" % i)
             for j in range(4):
-                copy = vcopy if j == 1 else scopy
+                copy = vcopy if j in HV.get(i, (1,)) else scopy
                 copy(h_grp[i][:, 128 * j : 128 * j + 128, :], h_ps[i][j][:].rearrange("p t n -> p n t"))
 
         def qh(i):
@@ -169,60 +201,58 @@ def tile_simplicialboundarycoboundarymessage_x2_kernel(
             h_sc[i] = sb("h_sc%d" % i, [P, 512], U8)
             quant(h_codes[i][:], h_sc[i][:], h_grp[i][:])
 
-        D, d_grp, d_codes, d_sc = {}, {}, {}, {}
+        D, d_grp, d_codes, d_sc, srt_t = {}, {}, {}, {}, {}
 
-        def td(k):
+        def rd(k):
             G, m = divmod(k, 2)
-            D[k] = {}
-            for g in range(2):
-                for tp in range(2):
-                    D[k][g, tp] = transposes(4 + 2 * g + tp, "dt%d%d%d" % (k, g, tp), inc_raw[m, G], 512 * g, tp)
+            srt_t[k] = reorder("ds%d" % k, inc_raw[m, G], REORD[k]) if k in REORD else None
 
-        def cd(k, v_share):
-            n = 0
-            for g in range(2):
-                d_grp[k, g] = grp_tile("d_grp%d%d" % (k, g))
-                for tp in range(2):
-                    copy_words(vcopy if n in v_share else scopy, d_grp[k, g], D[k][g, tp], tp)
-                    n += 1
+        def td(k, g):
+            G, m = divmod(k, 2)
+            D.setdefault(k, {})
+            for tp in range(2):
+                D[k][g, tp] = transposes(4 + 2 * g + tp, "dt%d%d%d" % (k, g, tp), inc_raw[m, G], 512 * g, tp, srt_t.get(k))
 
-        def qd(k):
-            for g in range(2):
-                d_codes[k, g] = sb("d_codes%d%d" % (k, g), [P, 512], U32)
-                d_sc[k, g] = sb("d_sc%d%d" % (k, g), [P, 512], U8)
-                quant(d_codes[k, g][:], d_sc[k, g][:], d_grp[k, g][:])
+        def cd(k, g):
+            d_grp[k, g] = grp_tile("d_grp%d%d" % (k, g))
+            for tp in range(2):
+                copy_words(vcopy if (2 * g + tp) in VC.get(k, ()) else scopy, d_grp[k, g], D[k][g, tp], tp)
+
+        def qd(k, g):
+            d_codes[k, g] = keep.tile([P, 512], U32, name="d_codes%d%d" % (k, g), tag="d_codes%d" % g, bufs=3, align_bytes=256)
+            d_sc[k, g] = keep.tile([P, 512], U8, name="d_sc%d%d" % (k, g), tag="d_sc%d" % g, bufs=3, align_bytes=256)
+            quant(d_codes[k, g][:], d_sc[k, g][:], d_grp[k, g][:])
 
         acc = {}
 
-        def mm(k, parts):
+        def mm(k, part, parts, ts):
             G, m = divmod(k, 2)
             width = F // parts
-            for h in range(parts):
-                cols = slice(width * h, width * h + width)
-                for t in range(4):
-                    rows = slice(128 * t, 128 * t + 128)
-                    if m == 0:
-                        acc[G, h, t] = bank(4 * h + t, "acc%d%d%d" % (G, h, t), [P, width])
-                    for g in range(2):
-                        nc.tensor.matmul_mx(
-                            out=acc[G, h, t][:],
-                            lhsT=d_codes[k, g][:, rows].bitcast(FP8X4),
-                            lhsT_scale=d_sc[k, g][:, rows],
-                            rhs=h_codes[2 * m + g][:, cols].bitcast(FP8X4),
-                            rhs_scale=h_sc[2 * m + g][:, cols],
-                            start=(m == 0 and g == 0),
-                            stop=(m == 1 and g == 1),
-                        )
+            cols = slice(width * part, width * part + width)
+            for t in ts:
+                rows = slice(128 * t, 128 * t + 128)
+                if m == 0:
+                    acc[G, part, t] = bank(4 * part + t, "acc%d%d%d" % (G, part, t), [P, width])
+                for g in range(2):
+                    nc.tensor.matmul_mx(
+                        out=acc[G, part, t][:],
+                        lhsT=d_codes[k, g][:, rows].bitcast(FP8X4),
+                        lhsT_scale=d_sc[k, g][:, rows],
+                        rhs=h_codes[2 * m + g][:, cols].bitcast(FP8X4),
+                        rhs_scale=h_sc[2 * m + g][:, cols],
+                        start=(m == 0 and g == 0),
+                        stop=(m == 1 and g == 1),
+                    )
 
         z_t, r_t, o_grp, o_codes, o_sc = {}, {}, {}, {}, {}
 
-        def adds(G, h, parts):
+        def adds(G, h, parts, ts=(0, 1, 2, 3)):
             width = F // parts
             cols = slice(width * h, width * h + width)
-            if h == 0:
+            if G not in z_t:
                 z_t[G] = keep.tile([P, 4, F], F32, name="z%d" % G, tag="z", bufs=2, align_bytes=256)
                 r_t[G] = sb("r%d" % G, [P, 4, F], F32)
-            for t in range(4):
+            for t in ts:
                 nc.vector.tensor_tensor(
                     out=z_t[G][:, t, cols], in0=acc[G, h, t][:], in1=x1_raw[G][:, t, cols], op=ALU.add
                 )
@@ -231,11 +261,21 @@ def tile_simplicialboundarycoboundarymessage_x2_kernel(
         def finish(G, h, parts):
             width = F // parts
             cols = slice(width * h, width * h + width)
-            if h == 0:
+            if G not in o_grp:
                 o_grp[G] = grp_tile("o_grp%d" % G)
                 o_codes[G] = sb("o_codes%d" % G, [P, F], U32)
                 o_sc[G] = sb("o_sc%d" % G, [P, F], U8)
-            nc.vector.tensor_copy(out=o_grp[G][:, cols, :], in_=r_t[G][:, :, cols].rearrange("p t f -> p f t"))
+            ze = ZE.get((G, h), "V")
+            step = 128
+            for f0 in range(width * h, width * h + width, step if ze == "G" else width):
+                cc = slice(f0, f0 + (step if ze == "G" else width))
+                dst, srcz = o_grp[G][:, cc, :], r_t[G][:, :, cc].rearrange("p t f -> p f t")
+                if ze == "V":
+                    nc.vector.tensor_copy(out=dst, in_=srcz)
+                elif ze == "S":
+                    nc.scalar.copy(out=dst, in_=srcz)
+                else:
+                    nc.gpsimd.tensor_scalar(out=dst, in0=srcz, scalar1=1.0, scalar2=0.0, op0=ALU.mult, op1=ALU.subtract)
             nc.sync.dma_start(
                 out=out_0[512 * G : 512 * G + 512, cols].rearrange("(p t) f -> p t f", t=4), in_=r_t[G][:, :, cols]
             )
@@ -249,60 +289,13 @@ def tile_simplicialboundarycoboundarymessage_x2_kernel(
                     in_=o_sc[G][32 * q : 32 * q + 4, cols].bitcast(I32),
                 )
 
-        with tc.manual_schedule():
-            tx(0)
-            tx(1)
-            cx(0)
-            qx(0)
-            cx(1)
-            s1(0)
-            tx(2)
-            qx(1)
-            ch(0)
-            s1(1)
-            cx(2)
-            qh(0)
-            tx(3)
-            qx(2)
-            ch(1)
-            s1(2)
-            cx(3)
-            qh(1)
-            td(0)
-            qx(3)
-            ch(2)
-            s1(3)
-            cd(0, (1,))
-            qh(2)
-            td(1)
-            qd(0)
-            ch(3)
-            mm(0, 1)
-            qh(3)
-            cd(1, (1,))
-            td(2)
-            qd(1)
-            mm(1, 1)
-            cd(2, ())
-            qd(2)
-            adds(0, 0, 1)
-            td(3)
-            mm(2, 1)
-            cd(3, ())
-            qd(3)
-            finish(0, 0, 1)
-            td(4)
-            mm(3, 1)
-            cd(4, ())
-            qd(4)
-            adds(1, 0, 1)
-            td(5)
-            mm(4, 2)
-            cd(5, (1, 3))
-            qd(5)
-            finish(1, 0, 1)
-            mm(5, 2)
-            adds(2, 0, 2)
-            finish(2, 0, 2)
-            adds(2, 1, 2)
-            finish(2, 1, 2)
+        def done_t(k):
+            cd(k, 0)
+            cd(k, 1)
+            qd(k, 0)
+            qd(k, 1)
+
+        fns = dict(tx=tx, cx=cx, qx=qx, s1=s1, ch=ch, qh=qh, rd=rd, td=td, cd=cd, qd=qd, mm=mm, ad=adds, fi=finish)
+        with tc.manual_schedule(engines={mybir.EngineType.PE, mybir.EngineType.SP}):
+            for name, args in SEQ:
+                fns[name](*args)

@@ -16,17 +16,11 @@ NE, NV, C, F = 1536, 1024, 512, 512
 FLOPS = 2 * (2 * NV * C * F) + 2 * (2 * NE * NV * F)
 
 P = 128
-REORD = {1: 'V', 2: 'V', 3: 'V', 4: 'V'}
-REORD_ENG = {}
-XREORD = ()
-SEQ = [('tx', (0,)), ('tx', (1,)), ('cx', (0,)), ('qx', (0,)), ('cx', (1,)), ('s1', (0,)), ('tx', (2,)), ('qx', (1,)), ('ch', (0,)), ('s1', (1,)), ('cx', (2,)), ('qh', (0,)), ('tx', (3,)), ('qx', (2,)), ('ch', (1,)), ('s1', (2,)), ('cx', (3,)), ('qh', (1,)), ('rd', (0,)), ('td', (0, 0)), ('td', (0, 1)), ('cd', (0, 0)), ('qd', (0, 0)), ('cd', (0, 1)), ('qd', (0, 1)), ('qx', (3,)), ('ch', (2,)), ('s1', (3,)), ('qh', (2,)), ('rd', (1,)), ('td', (1, 0)), ('td', (1, 1)), ('cd', (1, 0)), ('qd', (1, 0)), ('cd', (1, 1)), ('qd', (1, 1)), ('ch', (3,)), ('mm', (0, 0, 1, (0, 1, 2, 3))), ('qh', (3,)), ('rd', (2,)), ('td', (2, 0)), ('td', (2, 1)), ('cd', (2, 0)), ('qd', (2, 0)), ('cd', (2, 1)), ('qd', (2, 1)), ('mm', (1, 0, 1, (0, 1, 2, 3))), ('ad', (0, 0, 1, (0, 1, 2, 3))), ('rd', (3,)), ('td', (3, 0)), ('td', (3, 1)), ('cd', (3, 0)), ('qd', (3, 0)), ('cd', (3, 1)), ('qd', (3, 1)), ('mm', (2, 0, 1, (0, 1, 2, 3))), ('fi', (0, 0, 1)), ('rd', (4,)), ('td', (4, 0)), ('td', (4, 1)), ('cd', (4, 0)), ('qd', (4, 0)), ('cd', (4, 1)), ('qd', (4, 1)), ('mm', (3, 0, 1, (0, 1, 2, 3))), ('ad', (1, 0, 1, (0, 1, 2, 3))), ('rd', (5,)), ('td', (5, 0)), ('td', (5, 1)), ('cd', (5, 0)), ('qd', (5, 0)), ('cd', (5, 1)), ('qd', (5, 1)), ('mm', (4, 0, 2, (0, 1, 2, 3))), ('mm', (4, 1, 2, (0, 1, 2, 3))), ('fi', (1, 0, 1)), ('mm', (5, 0, 2, (0, 1, 2, 3))), ('ad', (2, 0, 2)), ('fi', (2, 0, 2)), ('mm', (5, 1, 2, (0, 1, 2, 3))), ('ad', (2, 1, 2)), ('fi', (2, 1, 2))]
-LASTPARTS = 2
-VC = {5: (1, 3)}
-XV = {}
-HV = {}
-ZE = {}
-XTB = [(0, 1), (2, 3), (0, 1), (6, 7)]
+RX = ()
+RD = (1, 2, 3, 4)
+ENG = {('cx', 0, 1): 'S', ('cx', 1, 1): 'V', ('cx', 2, 1): 'V', ('cx', 3, 1): 'S', ('ch', 0, 1): 'V', ('ch', 1, 1): 'S', ('ch', 2, 1): 'V', ('ch', 3, 1): 'V', ('cd', 5, 0, 1): 'V', ('cd', 5, 1, 1): 'S', ('cx', 1, 0): 'S', ('cd', 5, 0, 0): 'S', ('zc', 2, 256, 512): 'V', ('rd', 3, 1): 'S', ('cd', 1, 1, 1): 'S', ('ch', 1, 0): 'V', ('ch', 0, 3): 'S', ('ch', 0, 2): 'S', ('ch', 2, 0): 'V', ('ch', 0, 0): 'V', ('cd', 3, 0, 0): 'V', ('rd', 4, 1): 'V', ('cx', 0, 0): 'S'}
 X1LATE = 0
+ORDER = [('tx', 0, 0), ('cx', 0, 0), ('tx', 0, 1), ('cx', 0, 1), ('qx', 0), ('tx', 1, 0), ('cx', 1, 0), ('tx', 1, 1), ('cx', 1, 1), ('s1', 0, 0), ('ch', 0, 0), ('s1', 0, 2), ('qx', 1), ('s1', 0, 1), ('ch', 0, 2), ('s1', 0, 3), ('ch', 0, 1), ('ch', 0, 3), ('tx', 2, 1), ('cx', 2, 1), ('tx', 2, 0), ('cx', 2, 0), ('qh', 0), ('s1', 1, 0), ('s1', 1, 1), ('ch', 1, 0), ('s1', 1, 3), ('ch', 1, 1), ('s1', 1, 2), ('qx', 2), ('ch', 1, 3), ('tx', 3, 0), ('ch', 1, 2), ('tx', 3, 1), ('rd', 1, 0), ('cx', 3, 0), ('s1', 2, 0), ('qh', 1), ('s1', 2, 1), ('cx', 3, 1), ('s1', 2, 2), ('rd', 1, 1), ('s1', 2, 3), ('ch', 2, 2), ('qx', 3), ('td', 0, 0, 0), ('ch', 2, 3), ('ch', 2, 0), ('td', 0, 0, 1), ('cd', 0, 0, 0), ('td', 0, 1, 0), ('ch', 2, 1), ('cd', 0, 0, 1), ('td', 0, 1, 1), ('cd', 0, 1, 0), ('qd', 0, 0), ('s1', 3, 0), ('cd', 0, 1, 1), ('qh', 2), ('s1', 3, 1), ('ch', 3, 0), ('qd', 0, 1), ('s1', 3, 2), ('ch', 3, 2), ('rd', 2, 0), ('s1', 3, 3), ('ch', 3, 3), ('td', 1, 0, 0), ('ch', 3, 1), ('td', 1, 0, 1), ('cd', 1, 0, 0), ('rd', 2, 1), ('td', 1, 1, 0), ('td', 1, 1, 1), ('cd', 1, 0, 1), ('qh', 3), ('mm', 0, 0, 1, 0, 1), ('cd', 1, 1, 0), ('qd', 1, 0), ('mm', 0, 0, 1, 1, 2), ('cd', 1, 1, 1), ('rd', 3, 0), ('td', 2, 0, 0), ('rd', 3, 1), ('td', 2, 0, 1), ('qd', 1, 1), ('td', 2, 1, 0), ('td', 2, 1, 1), ('cd', 2, 1, 0), ('rd', 4, 0), ('mm', 0, 0, 1, 2, 3), ('cd', 2, 1, 1), ('mm', 0, 0, 1, 3, 4), ('rd', 4, 1), ('cd', 2, 0, 0), ('mm', 1, 0, 1, 0, 1), ('qd', 2, 1), ('cd', 2, 0, 1), ('mm', 1, 0, 1, 1, 2), ('ad', 0, 0, 1, 0), ('mm', 1, 0, 1, 3, 4), ('qd', 2, 0), ('si', 0, 0, 1, 0), ('mm', 1, 0, 1, 2, 3), ('ad', 0, 0, 1, 3), ('td', 3, 0, 0), ('ad', 0, 0, 1, 2), ('si', 0, 0, 1, 3), ('td', 3, 0, 1), ('td', 3, 1, 0), ('ad', 0, 0, 1, 1), ('si', 0, 0, 1, 2), ('td', 3, 1, 1), ('cd', 3, 0, 0), ('si', 0, 0, 1, 1), ('mm', 2, 0, 1, 2, 3), ('cd', 3, 1, 1), ('so', 0, 0, 256), ('zc', 0, 256, 512), ('mm', 2, 0, 1, 0, 1), ('cd', 3, 0, 1), ('mm', 2, 0, 1, 1, 2), ('zc', 0, 0, 256), ('cd', 3, 1, 0), ('mm', 2, 0, 1, 3, 4), ('qd', 3, 0), ('td', 4, 0, 0), ('qd', 3, 1), ('td', 4, 0, 1), ('cd', 4, 0, 0), ('td', 4, 1, 0), ('qo', 0, 256, 512), ('cd', 4, 0, 1), ('td', 4, 1, 1), ('qo', 0, 0, 256), ('mm', 3, 0, 1, 0, 1), ('cd', 4, 1, 1), ('qd', 4, 0), ('sp', 0, 0, 256), ('so', 0, 256, 512), ('mm', 3, 0, 1, 1, 2), ('cd', 4, 1, 0), ('ad', 1, 0, 1, 0), ('ad', 1, 0, 1, 1), ('si', 1, 0, 1, 0), ('td', 5, 0, 0), ('qd', 4, 1), ('mm', 3, 0, 1, 2, 3), ('cd', 5, 0, 0), ('mm', 3, 0, 1, 3, 4), ('si', 1, 0, 1, 1), ('ad', 1, 0, 1, 2), ('sp', 0, 256, 512), ('ad', 1, 0, 1, 3), ('si', 1, 0, 1, 2), ('td', 5, 0, 1), ('si', 1, 0, 1, 3), ('cd', 5, 0, 1), ('td', 5, 1, 1), ('cd', 5, 1, 1), ('td', 5, 1, 0), ('zc', 1, 0, 256), ('so', 1, 0, 256), ('mm', 4, 1, 2, 0, 1), ('cd', 5, 1, 0), ('qd', 5, 0), ('mm', 4, 0, 2, 0, 1), ('mm', 4, 0, 2, 1, 2), ('qd', 5, 1), ('mm', 4, 0, 2, 2, 3), ('qo', 1, 0, 256), ('zc', 1, 256, 512), ('mm', 4, 0, 2, 3, 4), ('sp', 1, 0, 256), ('so', 1, 256, 512), ('mm', 4, 1, 2, 3, 4), ('qo', 1, 256, 512), ('mm', 5, 0, 2, 0, 1), ('mm', 5, 0, 2, 1, 2), ('ad', 2, 0, 2, 0), ('mm', 5, 0, 2, 2, 3), ('ad', 2, 0, 2, 1), ('si', 2, 0, 2, 0), ('mm', 5, 0, 2, 3, 4), ('ad', 2, 0, 2, 2), ('si', 2, 0, 2, 1), ('mm', 4, 1, 2, 1, 2), ('ad', 2, 0, 2, 3), ('si', 2, 0, 2, 2), ('mm', 4, 1, 2, 2, 3), ('mm', 5, 1, 2, 0, 1), ('si', 2, 0, 2, 3), ('mm', 5, 1, 2, 1, 2), ('sp', 1, 256, 512), ('zc', 2, 0, 256), ('so', 2, 0, 256), ('mm', 5, 1, 2, 2, 3), ('mm', 5, 1, 2, 3, 4), ('ad', 2, 1, 2, 0), ('qo', 2, 0, 256), ('si', 2, 1, 2, 0), ('ad', 2, 1, 2, 1), ('ad', 2, 1, 2, 2), ('si', 2, 1, 2, 1), ('ad', 2, 1, 2, 3), ('si', 2, 1, 2, 2), ('sp', 2, 0, 256), ('si', 2, 1, 2, 3), ('zc', 2, 256, 512), ('so', 2, 256, 512), ('qo', 2, 256, 512), ('sp', 2, 256, 512)]
 
 
 def tile_simplicialboundarycoboundarymessage_x2_kernel(
@@ -130,16 +124,6 @@ def tile_simplicialboundarycoboundarymessage_x2_kernel(
                     nc.tensor.transpose(pt[:, 2 * tt + u, :], src_w, ident[:])
             return pt
 
-        def reorder(name, raw, eng):
-            width = raw.shape[2] // 2
-            t = keep.tile([P, 4, width], F32, name=name, tag="sorted%d" % width, bufs=3, align_bytes=256)
-            srcw = raw[:].rearrange("p t k -> p (t k)").bitcast(F32).rearrange("p (q w u) -> p q u w", u=2, w=128)
-            dst = t[:].rearrange("p t k -> p (t k)").rearrange("p (q u w) -> p q u w", u=2, w=128)
-            nq = 4 * width // 256
-            for i in range(2):
-                qs = slice(nq // 2 * i, nq // 2 * (i + 1))
-                (vcopy if eng == "V" else scopy)(dst[:, qs], srcw[:, qs])
-            return t
 
         def copy_words(copy, grp, pt, tp):
             dst = grp[:].rearrange("p r j -> p (r j)").bitcast(F32)[:, 512 * tp : 512 * tp + 512]
@@ -149,32 +133,46 @@ def tile_simplicialboundarycoboundarymessage_x2_kernel(
             )
 
         x_units = [(0, 0), (0, 1), (1, 0), (1, 1)]
-        X = {}
-        x_tbanks = XTB
+        x_tbanks = [(0, 1), (2, 3), (0, 1), (6, 7)]
         s_banks = [(4, 5, 6, 7), (2, 3, 4, 5), (0, 1, 2, 3), (0, 1, 2, 3)]
-
-        def tx(i):
-            m, g = x_units[i]
-            srt = reorder("xs%d" % i, x_raw[m, g], XREORD[i]) if i in XREORD else None
-            X[i] = [transposes(x_tbanks[i][tp], "xt%d%d" % (i, tp), x_raw[m, g], 0, tp, srt) for tp in range(2)]
-
-        x_grp, x_codes, x_sc = {}, {}, {}
+        xt, x_grp, x_codes, x_sc, x_srt = {}, {}, {}, {}, {}
         h_ps, h_grp, h_codes, h_sc = {}, {}, {}, {}
+        dt, d_grp, d_codes, d_sc, d_srt = {}, {}, {}, {}, {}
+        acc, z_t, r_t, o_grp, o_codes, o_sc = {}, {}, {}, {}, {}, {}
 
-        def cx(i):
-            x_grp[i] = grp_tile("x_grp%d" % i)
-            for tp in range(2):
-                copy_words(vcopy if tp in XV.get(i, (1,)) else scopy, x_grp[i], X[i][tp], tp)
+        def cp(key, default="S"):
+            return vcopy if ENG.get(key, default) == "V" else scopy
+
+        def reorder(key, name, store, k, raw, i):
+            width = raw.shape[2] // 2
+            if k not in store:
+                store[k] = keep.tile([P, 4, width], F32, name=name, tag="sorted%d" % width, bufs=2, align_bytes=256)
+            t = store[k]
+            srcw = raw[:].rearrange("p t k -> p (t k)").bitcast(F32).rearrange("p (q w u) -> p q u w", u=2, w=128)
+            dst = t[:].rearrange("p t k -> p (t k)").rearrange("p (q u w) -> p q u w", u=2, w=128)
+            nq = 4 * width // 256
+            qs = slice(nq // 2 * i, nq // 2 * (i + 1))
+            cp(key, "V")(dst[:, qs], srcw[:, qs])
+
+        def rx(i, half):
+            reorder(("rx", i, half), "xs%d" % i, x_srt, i, x_raw[x_units[i]], half)
+
+        def tx(i, tp):
+            xt[i, tp] = transposes(x_tbanks[i][tp], "xt%d%d" % (i, tp), x_raw[x_units[i]], 0, tp, x_srt.get(i))
+
+        def cx(i, tp):
+            if i not in x_grp:
+                x_grp[i] = grp_tile("x_grp%d" % i)
+            copy_words(cp(("cx", i, tp)), x_grp[i], xt[i, tp], tp)
 
         def qx(i):
             x_codes[i] = sb("x_codes%d" % i, [P, 512], U32)
             x_sc[i] = sb("x_sc%d" % i, [P, 512], U8)
             quant(x_codes[i][:], x_sc[i][:], x_grp[i][:])
 
-        def s1(i):
+        def s1(i, j):
             m, g = x_units[i]
-            h_ps[i] = []
-            for j in range(4):
+            if True:
                 hp = bank(s_banks[i][j], "hp%d%d" % (i, j), [P, 4, P])
                 cols = slice(128 * j, 128 * j + 128)
                 for t in range(4):
@@ -188,48 +186,42 @@ def tile_simplicialboundarycoboundarymessage_x2_kernel(
                         start=True,
                         stop=True,
                     )
-                h_ps[i].append(hp)
+                h_ps[i, j] = hp
 
-        def ch(i):
-            h_grp[i] = grp_tile("h_grp%d" % i)
-            for j in range(4):
-                copy = vcopy if j in HV.get(i, (1,)) else scopy
-                copy(h_grp[i][:, 128 * j : 128 * j + 128, :], h_ps[i][j][:].rearrange("p t n -> p n t"))
+        def ch(i, j):
+            if i not in h_grp:
+                h_grp[i] = grp_tile("h_grp%d" % i)
+            cp(("ch", i, j))(h_grp[i][:, 128 * j : 128 * j + 128, :], h_ps[i, j][:].rearrange("p t n -> p n t"))
 
         def qh(i):
             h_codes[i] = sb("h_codes%d" % i, [P, 512], U32)
             h_sc[i] = sb("h_sc%d" % i, [P, 512], U8)
             quant(h_codes[i][:], h_sc[i][:], h_grp[i][:])
 
-        D, d_grp, d_codes, d_sc, srt_t = {}, {}, {}, {}, {}
-
-        def rd(k):
+        def rd(k, half):
             G, m = divmod(k, 2)
-            srt_t[k] = reorder("ds%d" % k, inc_raw[m, G], REORD[k]) if k in REORD else None
+            reorder(("rd", k, half), "ds%d" % k, d_srt, k, inc_raw[m, G], half)
 
-        def td(k, g):
+        def td(k, g, tp):
             G, m = divmod(k, 2)
-            D.setdefault(k, {})
-            for tp in range(2):
-                D[k][g, tp] = transposes(4 + 2 * g + tp, "dt%d%d%d" % (k, g, tp), inc_raw[m, G], 512 * g, tp, srt_t.get(k))
+            if True:
+                dt[k, g, tp] = transposes(4 + 2 * g + tp, "dt%d%d%d" % (k, g, tp), inc_raw[m, G], 512 * g, tp, d_srt.get(k))
 
-        def cd(k, g):
-            d_grp[k, g] = grp_tile("d_grp%d%d" % (k, g))
-            for tp in range(2):
-                copy_words(vcopy if (2 * g + tp) in VC.get(k, ()) else scopy, d_grp[k, g], D[k][g, tp], tp)
+        def cd(k, g, tp):
+            if (k, g) not in d_grp:
+                d_grp[k, g] = grp_tile("d_grp%d%d" % (k, g))
+            copy_words(cp(("cd", k, g, tp)), d_grp[k, g], dt[k, g, tp], tp)
 
         def qd(k, g):
             d_codes[k, g] = keep.tile([P, 512], U32, name="d_codes%d%d" % (k, g), tag="d_codes%d" % g, bufs=3, align_bytes=256)
             d_sc[k, g] = keep.tile([P, 512], U8, name="d_sc%d%d" % (k, g), tag="d_sc%d" % g, bufs=3, align_bytes=256)
             quant(d_codes[k, g][:], d_sc[k, g][:], d_grp[k, g][:])
 
-        acc = {}
-
-        def mm(k, part, parts, ts):
+        def mm(k, part, parts, t0, t1):
             G, m = divmod(k, 2)
             width = F // parts
             cols = slice(width * part, width * part + width)
-            for t in ts:
+            for t in range(t0, t1):
                 rows = slice(128 * t, 128 * t + 128)
                 if m == 0:
                     acc[G, part, t] = bank(4 * part + t, "acc%d%d%d" % (G, part, t), [P, width])
@@ -244,58 +236,53 @@ def tile_simplicialboundarycoboundarymessage_x2_kernel(
                         stop=(m == 1 and g == 1),
                     )
 
-        z_t, r_t, o_grp, o_codes, o_sc = {}, {}, {}, {}, {}
-
-        def adds(G, h, parts, ts=(0, 1, 2, 3)):
+        def ad(G, h, parts, t):
             width = F // parts
             cols = slice(width * h, width * h + width)
             if G not in z_t:
                 z_t[G] = keep.tile([P, 4, F], F32, name="z%d" % G, tag="z", bufs=2, align_bytes=256)
-                r_t[G] = sb("r%d" % G, [P, 4, F], F32)
-            for t in ts:
-                nc.vector.tensor_tensor(
-                    out=z_t[G][:, t, cols], in0=acc[G, h, t][:], in1=x1_raw[G][:, t, cols], op=ALU.add
-                )
-                nc.scalar.activation(out=r_t[G][:, t, cols], in_=z_t[G][:, t, cols], func=ACT.Silu)
+            nc.vector.tensor_tensor(
+                out=z_t[G][:, t, cols], in0=acc[G, h, t][:], in1=x1_raw[G][:, t, cols], op=ALU.add
+            )
 
-        def finish(G, h, parts):
+        def si(G, h, parts, t):
             width = F // parts
             cols = slice(width * h, width * h + width)
+            if G not in r_t:
+                r_t[G] = sb("r%d" % G, [P, 4, F], F32)
+            nc.scalar.activation(out=r_t[G][:, t, cols], in_=z_t[G][:, t, cols], func=ACT.Silu)
+
+        def zc(G, f0, f1):
             if G not in o_grp:
                 o_grp[G] = grp_tile("o_grp%d" % G)
+            dst, srcz = o_grp[G][:, f0:f1, :], r_t[G][:, :, f0:f1].rearrange("p t f -> p f t")
+            if ENG.get(("zc", G, f0, f1), "V") == "G":
+                nc.gpsimd.tensor_scalar(out=dst, in0=srcz, scalar1=1.0, scalar2=0.0, op0=ALU.mult, op1=ALU.subtract)
+            else:
+                cp(("zc", G, f0, f1), "V")(dst, srcz)
+
+        def qo(G, f0, f1):
+            if G not in o_codes:
                 o_codes[G] = sb("o_codes%d" % G, [P, F], U32)
                 o_sc[G] = sb("o_sc%d" % G, [P, F], U8)
-            ze = ZE.get((G, h), "V")
-            step = 128
-            for f0 in range(width * h, width * h + width, step if ze == "G" else width):
-                cc = slice(f0, f0 + (step if ze == "G" else width))
-                dst, srcz = o_grp[G][:, cc, :], r_t[G][:, :, cc].rearrange("p t f -> p f t")
-                if ze == "V":
-                    nc.vector.tensor_copy(out=dst, in_=srcz)
-                elif ze == "S":
-                    nc.scalar.copy(out=dst, in_=srcz)
-                else:
-                    nc.gpsimd.tensor_scalar(out=dst, in0=srcz, scalar1=1.0, scalar2=0.0, op0=ALU.mult, op1=ALU.subtract)
+            quant(o_codes[G][:, f0:f1], o_sc[G][:, f0:f1], o_grp[G][:, f0:f1, :])
+
+        def so(G, f0, f1):
             nc.sync.dma_start(
-                out=out_0[512 * G : 512 * G + 512, cols].rearrange("(p t) f -> p t f", t=4), in_=r_t[G][:, :, cols]
+                out=out_0[512 * G : 512 * G + 512, f0:f1].rearrange("(p t) f -> p t f", t=4), in_=r_t[G][:, :, f0:f1]
             )
-            quant(o_codes[G][:, cols], o_sc[G][:, cols], o_grp[G][:, cols, :])
+
+        def sp(G, f0, f1):
             nc.sync.dma_start(
-                out=out_1[G].rearrange("p m t -> p (m t)").bitcast(I32)[:, cols], in_=o_codes[G][:, cols].bitcast(I32)
+                out=out_1[G].rearrange("p m t -> p (m t)").bitcast(I32)[:, f0:f1], in_=o_codes[G][:, f0:f1].bitcast(I32)
             )
             for q in range(4):
                 nc.sync.dma_start(
-                    out=out_2[G, 4 * q : 4 * q + 4, cols].bitcast(I32),
-                    in_=o_sc[G][32 * q : 32 * q + 4, cols].bitcast(I32),
+                    out=out_2[G, 4 * q : 4 * q + 4, f0:f1].bitcast(I32),
+                    in_=o_sc[G][32 * q : 32 * q + 4, f0:f1].bitcast(I32),
                 )
 
-        def done_t(k):
-            cd(k, 0)
-            cd(k, 1)
-            qd(k, 0)
-            qd(k, 1)
-
-        fns = dict(tx=tx, cx=cx, qx=qx, s1=s1, ch=ch, qh=qh, rd=rd, td=td, cd=cd, qd=qd, mm=mm, ad=adds, fi=finish)
-        with tc.manual_schedule(engines={mybir.EngineType.PE, mybir.EngineType.SP}):
-            for name, args in SEQ:
-                fns[name](*args)
+        fns = dict(rx=rx, tx=tx, cx=cx, qx=qx, s1=s1, ch=ch, qh=qh, rd=rd, td=td, cd=cd, qd=qd, mm=mm, ad=ad, si=si, zc=zc, qo=qo, so=so, sp=sp)
+        with tc.manual_schedule():
+            for key in ORDER:
+                fns[key[0]](*key[1:])

@@ -9,280 +9,456 @@ U32 = mybir.dt.uint32
 I32 = mybir.dt.int32
 U8 = mybir.dt.uint8
 FP8X4 = mybir.dt.float8_e4m3fn_x4
-ACT = mybir.ActivationFunctionType
-ALU = mybir.AluOpType
+SILU = mybir.ActivationFunctionType.Silu
+ADD = mybir.AluOpType.add
 
-NE, NV, C, F = 1536, 1024, 512, 512
-FLOPS = 2 * (2 * NV * C * F) + 2 * (2 * NE * NV * F)
+EDGES, CELLS, FEATURES, OUT = 1536, 1024, 512, 512
+FLOPS = 2 * (2 * CELLS * FEATURES * OUT) + 2 * (2 * EDGES * CELLS * OUT)
 
 P = 128
-RX = ()
-RD = (1, 2, 3, 4)
-ENG = {('cx', 0, 1): 'S', ('cx', 1, 1): 'V', ('cx', 2, 1): 'V', ('cx', 3, 1): 'S', ('ch', 0, 1): 'V', ('ch', 1, 1): 'S', ('ch', 2, 1): 'V', ('ch', 3, 1): 'V', ('cd', 5, 0, 1): 'V', ('cd', 5, 1, 1): 'S', ('cx', 1, 0): 'S', ('cd', 5, 0, 0): 'S', ('zc', 2, 256, 512): 'V', ('rd', 3, 1): 'S', ('cd', 1, 1, 1): 'S', ('ch', 1, 0): 'V', ('ch', 0, 3): 'S', ('ch', 0, 2): 'S', ('ch', 2, 0): 'V', ('ch', 0, 0): 'V', ('cd', 3, 0, 0): 'V', ('rd', 4, 1): 'V', ('cx', 0, 0): 'S'}
-X1LATE = 0
-ORDER = [('tx', 0, 0), ('cx', 0, 0), ('tx', 0, 1), ('cx', 0, 1), ('qx', 0), ('tx', 1, 0), ('cx', 1, 0), ('tx', 1, 1), ('cx', 1, 1), ('s1', 0, 0), ('ch', 0, 0), ('s1', 0, 2), ('qx', 1), ('s1', 0, 1), ('ch', 0, 2), ('s1', 0, 3), ('ch', 0, 1), ('ch', 0, 3), ('tx', 2, 1), ('cx', 2, 1), ('tx', 2, 0), ('cx', 2, 0), ('qh', 0), ('s1', 1, 0), ('s1', 1, 1), ('ch', 1, 0), ('s1', 1, 3), ('ch', 1, 1), ('s1', 1, 2), ('qx', 2), ('ch', 1, 3), ('tx', 3, 0), ('ch', 1, 2), ('tx', 3, 1), ('rd', 1, 0), ('cx', 3, 0), ('s1', 2, 0), ('qh', 1), ('s1', 2, 1), ('cx', 3, 1), ('s1', 2, 2), ('rd', 1, 1), ('s1', 2, 3), ('ch', 2, 2), ('qx', 3), ('td', 0, 0, 0), ('ch', 2, 3), ('ch', 2, 0), ('td', 0, 0, 1), ('cd', 0, 0, 0), ('td', 0, 1, 0), ('ch', 2, 1), ('cd', 0, 0, 1), ('td', 0, 1, 1), ('cd', 0, 1, 0), ('qd', 0, 0), ('s1', 3, 0), ('cd', 0, 1, 1), ('qh', 2), ('s1', 3, 1), ('ch', 3, 0), ('qd', 0, 1), ('s1', 3, 2), ('ch', 3, 2), ('rd', 2, 0), ('s1', 3, 3), ('ch', 3, 3), ('td', 1, 0, 0), ('ch', 3, 1), ('td', 1, 0, 1), ('cd', 1, 0, 0), ('rd', 2, 1), ('td', 1, 1, 0), ('td', 1, 1, 1), ('cd', 1, 0, 1), ('qh', 3), ('mm', 0, 0, 1, 0, 1), ('cd', 1, 1, 0), ('qd', 1, 0), ('mm', 0, 0, 1, 1, 2), ('cd', 1, 1, 1), ('rd', 3, 0), ('td', 2, 0, 0), ('rd', 3, 1), ('td', 2, 0, 1), ('qd', 1, 1), ('td', 2, 1, 0), ('td', 2, 1, 1), ('cd', 2, 1, 0), ('rd', 4, 0), ('mm', 0, 0, 1, 2, 3), ('cd', 2, 1, 1), ('mm', 0, 0, 1, 3, 4), ('rd', 4, 1), ('cd', 2, 0, 0), ('mm', 1, 0, 1, 0, 1), ('qd', 2, 1), ('cd', 2, 0, 1), ('mm', 1, 0, 1, 1, 2), ('ad', 0, 0, 1, 0), ('mm', 1, 0, 1, 3, 4), ('qd', 2, 0), ('si', 0, 0, 1, 0), ('mm', 1, 0, 1, 2, 3), ('ad', 0, 0, 1, 3), ('td', 3, 0, 0), ('ad', 0, 0, 1, 2), ('si', 0, 0, 1, 3), ('td', 3, 0, 1), ('td', 3, 1, 0), ('ad', 0, 0, 1, 1), ('si', 0, 0, 1, 2), ('td', 3, 1, 1), ('cd', 3, 0, 0), ('si', 0, 0, 1, 1), ('mm', 2, 0, 1, 2, 3), ('cd', 3, 1, 1), ('so', 0, 0, 256), ('zc', 0, 256, 512), ('mm', 2, 0, 1, 0, 1), ('cd', 3, 0, 1), ('mm', 2, 0, 1, 1, 2), ('zc', 0, 0, 256), ('cd', 3, 1, 0), ('mm', 2, 0, 1, 3, 4), ('qd', 3, 0), ('td', 4, 0, 0), ('qd', 3, 1), ('td', 4, 0, 1), ('cd', 4, 0, 0), ('td', 4, 1, 0), ('qo', 0, 256, 512), ('cd', 4, 0, 1), ('td', 4, 1, 1), ('qo', 0, 0, 256), ('mm', 3, 0, 1, 0, 1), ('cd', 4, 1, 1), ('qd', 4, 0), ('sp', 0, 0, 256), ('so', 0, 256, 512), ('mm', 3, 0, 1, 1, 2), ('cd', 4, 1, 0), ('ad', 1, 0, 1, 0), ('ad', 1, 0, 1, 1), ('si', 1, 0, 1, 0), ('td', 5, 0, 0), ('qd', 4, 1), ('mm', 3, 0, 1, 2, 3), ('cd', 5, 0, 0), ('mm', 3, 0, 1, 3, 4), ('si', 1, 0, 1, 1), ('ad', 1, 0, 1, 2), ('sp', 0, 256, 512), ('ad', 1, 0, 1, 3), ('si', 1, 0, 1, 2), ('td', 5, 0, 1), ('si', 1, 0, 1, 3), ('cd', 5, 0, 1), ('td', 5, 1, 1), ('cd', 5, 1, 1), ('td', 5, 1, 0), ('zc', 1, 0, 256), ('so', 1, 0, 256), ('mm', 4, 1, 2, 0, 1), ('cd', 5, 1, 0), ('qd', 5, 0), ('mm', 4, 0, 2, 0, 1), ('mm', 4, 0, 2, 1, 2), ('qd', 5, 1), ('mm', 4, 0, 2, 2, 3), ('qo', 1, 0, 256), ('zc', 1, 256, 512), ('mm', 4, 0, 2, 3, 4), ('sp', 1, 0, 256), ('so', 1, 256, 512), ('mm', 4, 1, 2, 3, 4), ('qo', 1, 256, 512), ('mm', 5, 0, 2, 0, 1), ('mm', 5, 0, 2, 1, 2), ('ad', 2, 0, 2, 0), ('mm', 5, 0, 2, 2, 3), ('ad', 2, 0, 2, 1), ('si', 2, 0, 2, 0), ('mm', 5, 0, 2, 3, 4), ('ad', 2, 0, 2, 2), ('si', 2, 0, 2, 1), ('mm', 4, 1, 2, 1, 2), ('ad', 2, 0, 2, 3), ('si', 2, 0, 2, 2), ('mm', 4, 1, 2, 2, 3), ('mm', 5, 1, 2, 0, 1), ('si', 2, 0, 2, 3), ('mm', 5, 1, 2, 1, 2), ('sp', 1, 256, 512), ('zc', 2, 0, 256), ('so', 2, 0, 256), ('mm', 5, 1, 2, 2, 3), ('mm', 5, 1, 2, 3, 4), ('ad', 2, 1, 2, 0), ('qo', 2, 0, 256), ('si', 2, 1, 2, 0), ('ad', 2, 1, 2, 1), ('ad', 2, 1, 2, 2), ('si', 2, 1, 2, 1), ('ad', 2, 1, 2, 3), ('si', 2, 1, 2, 2), ('sp', 2, 0, 256), ('si', 2, 1, 2, 3), ('zc', 2, 256, 512), ('so', 2, 256, 512), ('qo', 2, 256, 512), ('sp', 2, 256, 512)]
+PACK = 4
+K_PASS = P * PACK
+HALF_PASS = K_PASS // 2
+
+ALL, LEFT, RIGHT = slice(0, 512), slice(0, 256), slice(256, 512)
+
+VECTOR, SCALAR = "vector", "scalar"
+
+ARRANGED = (1, 2, 3, 4)
+
+BUFFERS = {"grouped": 6, "sorted": 2, "inc_grouped": 3, "inc_codes": 3, "inc_plane": 3, "z": 2}
 
 
 def tile_simplicialboundarycoboundarymessage_x2_kernel(
     tc, x0, x1, x2, inc_down, inc_up, w0_words, w0_scales, w2_words, w2_scales, out_0, out_1, out_2
 ):
     nc = tc.nc
-    cells = [x0, x2]
-    incs = [inc_down, inc_up]
-    wwords = [w0_words, w2_words]
-    wscales = [w0_scales, w2_scales]
+    cells, incidences = (x0, x2), (inc_down, inc_up)
+    weight_words, weight_scales = (w0_words, w2_words), (w0_scales, w2_scales)
 
     with ExitStack() as ctx:
         keep = ctx.enter_context(tc.tile_pool(name="keep", bufs=1))
+        turn = ctx.enter_context(tc.tile_pool(name="turn", bufs=1))
         psum = ctx.enter_context(tc.psum_pool(name="psum", bufs=1))
 
-        def sb(name, shape, dtype):
+        def fixed(name, shape, dtype):
             return keep.tile(shape, dtype, name=name, tag=name, align_bytes=256)
 
-        grp_pool = ctx.enter_context(tc.tile_pool(name="grp_pool", bufs=8))
+        def shared(name, tag, shape, dtype):
+            return turn.tile(shape, dtype, name=name, tag=tag, bufs=BUFFERS[tag], align_bytes=256)
 
-        def grp_tile(name):
-            return grp_pool.tile([P, 512, 4], BF16, name=name, tag="grp", align_bytes=256)
+        def bank(number, name, shape):
+            return psum.tile(shape, F32, name=name, tag="bank%d" % number)
 
-        def bank(b, name, shape):
-            return psum.tile(shape, F32, name=name, tag="bank%d" % b)
-
-        warm = sb("warm", [P, 1], F32)
-        nc.vector.memset(warm[:], 0.0)
-        ident = sb("ident", [P, P], F32)
-        make_identity(nc, ident[:])
-        w_codes = []
-        w_sc = []
-        for m in range(2):
-            w_codes.append(sb("w_codes%d" % m, [P, F], U32))
-            plane = sb("w_sc%d" % m, [P, F], U8)
+        zero = fixed("zero", [P, 1], F32)
+        nc.vector.memset(zero[:], 0.0)
+        identity = fixed("identity", [P, P], F32)
+        make_identity(nc, identity[:])
+        weight_codes, weight_planes = [], []
+        for side in range(2):
+            weight_codes.append(fixed("weight_codes%d" % side, [P, OUT], U32))
+            plane = fixed("weight_plane%d" % side, [P, OUT], U8)
             nc.vector.memset(plane[:].bitcast(I32), 0)
-            w_sc.append(plane)
-        nc.scalar.activation(out=warm[:], in_=warm[:], func=ACT.Silu)
+            weight_planes.append(plane)
+        nc.scalar.activation(out=zero[:], in_=zero[:], func=SILU)
 
-        x_raw = {}
-        for m in range(2):
-            for g in range(2):
-                raw = sb("x_raw%d%d" % (m, g), [P, 4, C], BF16)
-                x_raw[m, g] = raw
-                src = cells[m][512 * g : 512 * g + 512, :].rearrange("(p t) c -> p t c", t=4)
-                if m == 0 and g == 0:
-                    nc.sync.dma_start(out=raw[:, 0:2, :], in_=src[:, 0:2, :])
-                    nc.sync.dma_start(out=raw[:, 2:4, :], in_=src[:, 2:4, :])
-                else:
-                    nc.sync.dma_start(out=raw[:], in_=src)
-                if g == 0:
-                    for q in range(4):
-                        nc.sync.dma_start(
-                            out=w_sc[m][32 * q : 32 * q + 4, :].bitcast(I32),
-                            in_=wscales[m][0, 4 * q : 4 * q + 4, :].bitcast(I32),
-                        )
-            nc.sync.dma_start(out=w_codes[m][:].bitcast(I32), in_=wwords[m][0].rearrange("p n t -> p (n t)").bitcast(I32))
-        inc_raw = {}
-        x1_raw = {}
-        for G in range(3):
-            for m in range(2):
-                raw = sb("inc_raw%d%d" % (m, G), [P, 4, NV], BF16)
-                inc_raw[m, G] = raw
-                src = incs[m][512 * G : 512 * G + 512, :].rearrange("(p t) k -> p t k", t=4)
-                if G == 0:
-                    nc.sync.dma_start(out=raw[:, 0:2, :], in_=src[:, 0:2, :])
-                    nc.sync.dma_start(out=raw[:, 2:4, :], in_=src[:, 2:4, :])
-                else:
-                    nc.sync.dma_start(out=raw[:], in_=src)
-            if X1LATE and G == 0:
-                continue
-            for G1 in ((0, 1) if X1LATE and G == 1 else (G,)):
-              t1 = sb("x1_raw%d" % G1, [P, 4, F], BF16)
-              x1_raw[G1] = t1
-              nc.sync.dma_start(out=t1[:], in_=x1[512 * G1 : 512 * G1 + 512, :].rearrange("(p t) f -> p t f", t=4))
+        def by_four(rows):
+            return rows.rearrange("(p t) c -> p t c", t=PACK)
 
-        def scopy(out, in_):
-            nc.scalar.copy(out=out, in_=in_)
+        x_raw, inc_raw, x1_raw = {}, {}, {}
 
-        def vcopy(out, in_):
-            nc.vector.tensor_copy(out=out, in_=in_)
+        def load_cells(i, slots=range(0, 4)):
+            if i not in x_raw:
+                x_raw[i] = fixed("x_raw%d" % i, [P, PACK, FEATURES], BF16)
+            start = K_PASS * (i % 2)
+            source = by_four(cells[i // 2][start : start + K_PASS, :])
+            nc.sync.dma_start(out=x_raw[i][:, slots.start : slots.stop, :], in_=source[:, slots.start : slots.stop, :])
 
-        def quant(codes, sc, grp):
+        def load_weight_scales(side):
+            for q in range(4):
+                nc.sync.dma_start(
+                    out=weight_planes[side][32 * q : 32 * q + 4, :].bitcast(I32),
+                    in_=weight_scales[side][0, 4 * q : 4 * q + 4, :].bitcast(I32),
+                )
+
+        def load_weight_words(side):
+            nc.sync.dma_start(
+                out=weight_codes[side][:].bitcast(I32),
+                in_=weight_words[side][0].rearrange("p n t -> p (n t)").bitcast(I32),
+            )
+
+        def load_incidence(k):
+            inc_raw[k] = fixed("inc_raw%d" % k, [P, PACK, CELLS], BF16)
+            start = K_PASS * (k // 2)
+            nc.sync.dma_start(out=inc_raw[k][:], in_=by_four(incidences[k % 2][start : start + K_PASS, :]))
+
+        def load_x1(block):
+            x1_raw[block] = fixed("x1_raw%d" % block, [P, PACK, OUT], BF16)
+            nc.sync.dma_start(out=x1_raw[block][:], in_=by_four(x1[K_PASS * block : K_PASS * block + K_PASS, :]))
+
+        load_cells(0, range(0, 2))
+        load_cells(0, range(2, 4))
+        load_cells(1)
+        load_weight_scales(0)
+        load_weight_words(0)
+        load_cells(2)
+        load_cells(3)
+        load_weight_words(1)
+        load_incidence(0)
+        load_weight_scales(1)
+        load_incidence(1)
+        load_incidence(2)
+        load_incidence(3)
+        load_x1(0)
+        load_incidence(4)
+        load_incidence(5)
+        load_x1(1)
+        load_x1(2)
+
+        def copy(engine, out, in_):
+            if engine == VECTOR:
+                nc.vector.tensor_copy(out=out, in_=in_)
+            else:
+                nc.scalar.copy(out=out, in_=in_)
+
+        def quantize(codes, scales, grouped):
             nc.vector.quantize_mx(
-                out=codes.bitcast(FP8X4), scales=sc, in_=grp.rearrange("p r j -> p (r j)")
+                out=codes.bitcast(FP8X4), scales=scales, in_=grouped.rearrange("p c t -> p (c t)")
             )
 
-        def transposes(b, name, raw, k0, tp, sorted_words=None):
-            words = raw[:].rearrange("p t k -> p (t k)").bitcast(F32)
-            width = raw.shape[2] // 2
-            pt = bank(b, name, [P, 4, P])
-            for tt in range(2):
+        def as_words(tile):
+            return tile[:].rearrange("p t k -> p (t k)").bitcast(F32)
+
+        def transpose_pair(out, source_words, pair):
+            for a in range(2):
                 for u in range(2):
-                    t = 2 * tp + tt
-                    if sorted_words is not None:
-                        w0 = k0 // 2 + 128 * u
-                        src_w = sorted_words[:, t, w0 : w0 + 128]
-                    else:
-                        w0 = t * width + k0 // 2 + u
-                        src_w = words[:, w0 : w0 + 255 : 2]
-                    nc.tensor.transpose(pt[:, 2 * tt + u, :], src_w, ident[:])
-            return pt
+                    nc.tensor.transpose(out[:, 2 * a + u, :], source_words(2 * pair + a, u), identity[:])
 
-
-        def copy_words(copy, grp, pt, tp):
-            dst = grp[:].rearrange("p r j -> p (r j)").bitcast(F32)[:, 512 * tp : 512 * tp + 512]
+        def empty_pair(engine, grouped, transposed, pair):
+            words = grouped.rearrange("p c t -> p (c t)").bitcast(F32)[:, K_PASS * pair : K_PASS * pair + K_PASS]
             copy(
-                dst.rearrange("p (a r u) -> p a r u", a=2, u=2),
-                pt[:].rearrange("p (a u) r -> p a r u", u=2),
+                engine,
+                words.rearrange("p (a m u) -> p a m u", a=2, u=2),
+                transposed[:].rearrange("p (a u) m -> p a m u", u=2),
             )
 
-        x_units = [(0, 0), (0, 1), (1, 0), (1, 1)]
-        x_tbanks = [(0, 1), (2, 3), (0, 1), (6, 7)]
-        s_banks = [(4, 5, 6, 7), (2, 3, 4, 5), (0, 1, 2, 3), (0, 1, 2, 3)]
-        xt, x_grp, x_codes, x_sc, x_srt = {}, {}, {}, {}, {}
-        h_ps, h_grp, h_codes, h_sc = {}, {}, {}, {}
-        dt, d_grp, d_codes, d_sc, d_srt = {}, {}, {}, {}, {}
-        acc, z_t, r_t, o_grp, o_codes, o_sc = {}, {}, {}, {}, {}, {}
+        x_banks = ((0, 1), (2, 3), (0, 1), (6, 7))
+        h_banks = ((4, 5, 6, 7), (2, 3, 4, 5), (0, 1, 2, 3), (0, 1, 2, 3))
+        x_turned, x_grouped, x_codes, x_planes = {}, {}, {}, {}
+        h_sums, h_grouped, h_codes, h_planes = {}, {}, {}, {}
 
-        def cp(key, default="S"):
-            return vcopy if ENG.get(key, default) == "V" else scopy
+        def transpose_cells(i):
+            words = as_words(x_raw[i])
+            for pair in range(2):
+                x_turned[i, pair] = bank(x_banks[i][pair], "x_turned%d%d" % (i, pair), [P, 4, P])
 
-        def reorder(key, name, store, k, raw, i):
-            width = raw.shape[2] // 2
-            if k not in store:
-                store[k] = keep.tile([P, 4, width], F32, name=name, tag="sorted%d" % width, bufs=2, align_bytes=256)
-            t = store[k]
-            srcw = raw[:].rearrange("p t k -> p (t k)").bitcast(F32).rearrange("p (q w u) -> p q u w", u=2, w=128)
-            dst = t[:].rearrange("p t k -> p (t k)").rearrange("p (q u w) -> p q u w", u=2, w=128)
-            nq = 4 * width // 256
-            qs = slice(nq // 2 * i, nq // 2 * (i + 1))
-            cp(key, "V")(dst[:, qs], srcw[:, qs])
+                def every_second_word(t, u):
+                    first = HALF_PASS * t + u
+                    return words[:, first : first + HALF_PASS - 1 : 2]
 
-        def rx(i, half):
-            reorder(("rx", i, half), "xs%d" % i, x_srt, i, x_raw[x_units[i]], half)
+                transpose_pair(x_turned[i, pair], every_second_word, pair)
 
-        def tx(i, tp):
-            xt[i, tp] = transposes(x_tbanks[i][tp], "xt%d%d" % (i, tp), x_raw[x_units[i]], 0, tp, x_srt.get(i))
+        def empty_cells(engine, i, pair):
+            if i not in x_grouped:
+                x_grouped[i] = shared("x_grouped%d" % i, "grouped", [P, K_PASS, PACK], BF16)
+            empty_pair(engine, x_grouped[i][:], x_turned[i, pair], pair)
 
-        def cx(i, tp):
-            if i not in x_grp:
-                x_grp[i] = grp_tile("x_grp%d" % i)
-            copy_words(cp(("cx", i, tp)), x_grp[i], xt[i, tp], tp)
+        def quantize_cells(i):
+            x_codes[i] = fixed("x_codes%d" % i, [P, K_PASS], U32)
+            x_planes[i] = fixed("x_plane%d" % i, [P, K_PASS], U8)
+            quantize(x_codes[i][:], x_planes[i][:], x_grouped[i][:])
 
-        def qx(i):
-            x_codes[i] = sb("x_codes%d" % i, [P, 512], U32)
-            x_sc[i] = sb("x_sc%d" % i, [P, 512], U8)
-            quant(x_codes[i][:], x_sc[i][:], x_grp[i][:])
-
-        def s1(i, j):
-            m, g = x_units[i]
-            if True:
-                hp = bank(s_banks[i][j], "hp%d%d" % (i, j), [P, 4, P])
-                cols = slice(128 * j, 128 * j + 128)
+        def project(i, quarters):
+            side = i // 2
+            for j in quarters:
+                h_sums[i, j] = bank(h_banks[i][j], "h_sums%d%d" % (i, j), [P, PACK, P])
+                columns = slice(128 * j, 128 * j + 128)
                 for t in range(4):
                     rows = slice(128 * t, 128 * t + 128)
                     nc.tensor.matmul_mx(
-                        out=hp[:, t, :],
+                        out=h_sums[i, j][:, t, :],
                         lhsT=x_codes[i][:, rows].bitcast(FP8X4),
-                        lhsT_scale=x_sc[i][:, rows],
-                        rhs=w_codes[m][:, cols].bitcast(FP8X4),
-                        rhs_scale=w_sc[m][:, cols],
+                        lhsT_scale=x_planes[i][:, rows],
+                        rhs=weight_codes[side][:, columns].bitcast(FP8X4),
+                        rhs_scale=weight_planes[side][:, columns],
                         start=True,
                         stop=True,
                     )
-                h_ps[i, j] = hp
 
-        def ch(i, j):
-            if i not in h_grp:
-                h_grp[i] = grp_tile("h_grp%d" % i)
-            cp(("ch", i, j))(h_grp[i][:, 128 * j : 128 * j + 128, :], h_ps[i, j][:].rearrange("p t n -> p n t"))
+        def empty_hidden(engine, i, j):
+            if i not in h_grouped:
+                h_grouped[i] = shared("h_grouped%d" % i, "grouped", [P, OUT, PACK], BF16)
+            copy(engine, h_grouped[i][:, 128 * j : 128 * j + 128, :], h_sums[i, j][:].rearrange("p t n -> p n t"))
 
-        def qh(i):
-            h_codes[i] = sb("h_codes%d" % i, [P, 512], U32)
-            h_sc[i] = sb("h_sc%d" % i, [P, 512], U8)
-            quant(h_codes[i][:], h_sc[i][:], h_grp[i][:])
+        def quantize_hidden(i):
+            h_codes[i] = fixed("h_codes%d" % i, [P, OUT], U32)
+            h_planes[i] = fixed("h_plane%d" % i, [P, OUT], U8)
+            quantize(h_codes[i][:], h_planes[i][:], h_grouped[i][:])
 
-        def rd(k, half):
-            G, m = divmod(k, 2)
-            reorder(("rd", k, half), "ds%d" % k, d_srt, k, inc_raw[m, G], half)
+        inc_sorted, inc_turned, inc_grouped, inc_codes, inc_planes, sums = {}, {}, {}, {}, {}, {}
 
-        def td(k, g, tp):
-            G, m = divmod(k, 2)
-            if True:
-                dt[k, g, tp] = transposes(4 + 2 * g + tp, "dt%d%d%d" % (k, g, tp), inc_raw[m, G], 512 * g, tp, d_srt.get(k))
+        def arrange_words(engine, k, half):
+            if k not in inc_sorted:
+                inc_sorted[k] = shared("inc_sorted%d" % k, "sorted", [P, PACK, CELLS // 2], F32)
+            source = as_words(inc_raw[k]).rearrange("p (s w u) -> p s u w", u=2, w=P)
+            target = inc_sorted[k][:].rearrange("p t k -> p (t k)").rearrange("p (s u w) -> p s u w", u=2, w=P)
+            runs = slice(4 * half, 4 * half + 4)
+            copy(engine, target[:, runs], source[:, runs])
 
-        def cd(k, g, tp):
-            if (k, g) not in d_grp:
-                d_grp[k, g] = grp_tile("d_grp%d%d" % (k, g))
-            copy_words(cp(("cd", k, g, tp)), d_grp[k, g], dt[k, g, tp], tp)
+        def transpose_incidence(k, g):
+            words = as_words(inc_raw[k])
+            for pair in range(2):
+                inc_turned[k, g, pair] = bank(4 + 2 * g + pair, "inc_turned%d%d%d" % (k, g, pair), [P, 4, P])
 
-        def qd(k, g):
-            d_codes[k, g] = keep.tile([P, 512], U32, name="d_codes%d%d" % (k, g), tag="d_codes%d" % g, bufs=3, align_bytes=256)
-            d_sc[k, g] = keep.tile([P, 512], U8, name="d_sc%d%d" % (k, g), tag="d_sc%d" % g, bufs=3, align_bytes=256)
-            quant(d_codes[k, g][:], d_sc[k, g][:], d_grp[k, g][:])
+                def every_second_word(t, u):
+                    first = (CELLS // 2) * t + HALF_PASS * g + u
+                    return words[:, first : first + HALF_PASS - 1 : 2]
 
-        def mm(k, part, parts, t0, t1):
-            G, m = divmod(k, 2)
-            width = F // parts
-            cols = slice(width * part, width * part + width)
-            for t in range(t0, t1):
-                rows = slice(128 * t, 128 * t + 128)
-                if m == 0:
-                    acc[G, part, t] = bank(4 * part + t, "acc%d%d%d" % (G, part, t), [P, width])
+                def sorted_words(t, u):
+                    first = HALF_PASS * g + P * u
+                    return inc_sorted[k][:, t, first : first + P]
+
+                transpose_pair(inc_turned[k, g, pair], sorted_words if k in ARRANGED else every_second_word, pair)
+
+        def empty_incidence(engine, k, g, pair):
+            if k not in inc_grouped:
+                inc_grouped[k] = shared("inc_grouped%d" % k, "inc_grouped", [P, 2 * K_PASS, PACK], BF16)
+            empty_pair(engine, inc_grouped[k][:, K_PASS * g : K_PASS * g + K_PASS, :], inc_turned[k, g, pair], pair)
+
+        def quantize_incidence(k, first, end):
+            if k not in inc_codes:
+                inc_codes[k] = shared("inc_codes%d" % k, "inc_codes", [P, 2 * K_PASS], U32)
+                inc_planes[k] = shared("inc_plane%d" % k, "inc_plane", [P, 2 * K_PASS], U8)
+            columns = slice(first, end)
+            quantize(inc_codes[k][:, columns], inc_planes[k][:, columns], inc_grouped[k][:, columns, :])
+
+        def multiply(k, columns, slots):
+            block, side = divmod(k, 2)
+            for t in slots:
+                key = (block, columns.start, t)
+                if side == 0:
+                    number = t + (4 if columns.start > 0 else 0)
+                    sums[key] = bank(number, "sums%d_%d_%d" % key, [P, columns.stop - columns.start])
                 for g in range(2):
+                    rows = slice(K_PASS * g + 128 * t, K_PASS * g + 128 * t + 128)
                     nc.tensor.matmul_mx(
-                        out=acc[G, part, t][:],
-                        lhsT=d_codes[k, g][:, rows].bitcast(FP8X4),
-                        lhsT_scale=d_sc[k, g][:, rows],
-                        rhs=h_codes[2 * m + g][:, cols].bitcast(FP8X4),
-                        rhs_scale=h_sc[2 * m + g][:, cols],
-                        start=(m == 0 and g == 0),
-                        stop=(m == 1 and g == 1),
+                        out=sums[key][:],
+                        lhsT=inc_codes[k][:, rows].bitcast(FP8X4),
+                        lhsT_scale=inc_planes[k][:, rows],
+                        rhs=h_codes[2 * side + g][:, columns].bitcast(FP8X4),
+                        rhs_scale=h_planes[2 * side + g][:, columns],
+                        start=(side == 0 and g == 0),
+                        stop=(side == 1 and g == 1),
                     )
 
-        def ad(G, h, parts, t):
-            width = F // parts
-            cols = slice(width * h, width * h + width)
-            if G not in z_t:
-                z_t[G] = keep.tile([P, 4, F], F32, name="z%d" % G, tag="z", bufs=2, align_bytes=256)
+        z, result, out_grouped, out_codes, out_planes = {}, {}, {}, {}, {}
+
+        def add_x1(block, columns, t):
+            if block not in z:
+                z[block] = shared("z%d" % block, "z", [P, PACK, OUT], F32)
             nc.vector.tensor_tensor(
-                out=z_t[G][:, t, cols], in0=acc[G, h, t][:], in1=x1_raw[G][:, t, cols], op=ALU.add
+                out=z[block][:, t, columns],
+                in0=sums[block, columns.start, t][:],
+                in1=x1_raw[block][:, t, columns],
+                op=ADD,
             )
 
-        def si(G, h, parts, t):
-            width = F // parts
-            cols = slice(width * h, width * h + width)
-            if G not in r_t:
-                r_t[G] = sb("r%d" % G, [P, 4, F], F32)
-            nc.scalar.activation(out=r_t[G][:, t, cols], in_=z_t[G][:, t, cols], func=ACT.Silu)
+        def silu(block, columns, t):
+            if block not in result:
+                result[block] = fixed("result%d" % block, [P, PACK, OUT], F32)
+            nc.scalar.activation(
+                out=result[block][:, t : t + 2, columns],
+                in_=z[block][:, t : t + 2, columns],
+                func=SILU,
+                bias=zero[:],
+            )
 
-        def zc(G, f0, f1):
-            if G not in o_grp:
-                o_grp[G] = grp_tile("o_grp%d" % G)
-            dst, srcz = o_grp[G][:, f0:f1, :], r_t[G][:, :, f0:f1].rearrange("p t f -> p f t")
-            if ENG.get(("zc", G, f0, f1), "V") == "G":
-                nc.gpsimd.tensor_scalar(out=dst, in0=srcz, scalar1=1.0, scalar2=0.0, op0=ALU.mult, op1=ALU.subtract)
-            else:
-                cp(("zc", G, f0, f1), "V")(dst, srcz)
+        def interleave(engine, block, columns):
+            if block not in out_grouped:
+                out_grouped[block] = shared("out_grouped%d" % block, "grouped", [P, OUT, PACK], BF16)
+            copy(engine, out_grouped[block][:, columns, :], result[block][:, :, columns].rearrange("p t f -> p f t"))
 
-        def qo(G, f0, f1):
-            if G not in o_codes:
-                o_codes[G] = sb("o_codes%d" % G, [P, F], U32)
-                o_sc[G] = sb("o_sc%d" % G, [P, F], U8)
-            quant(o_codes[G][:, f0:f1], o_sc[G][:, f0:f1], o_grp[G][:, f0:f1, :])
+        def quantize_result(block, columns):
+            if block not in out_codes:
+                out_codes[block] = fixed("out_codes%d" % block, [P, OUT], U32)
+                out_planes[block] = fixed("out_plane%d" % block, [P, OUT], U8)
+            quantize(out_codes[block][:, columns], out_planes[block][:, columns], out_grouped[block][:, columns, :])
 
-        def so(G, f0, f1):
+        def store_result(block, columns):
+            rows = slice(K_PASS * block, K_PASS * block + K_PASS)
+            nc.sync.dma_start(out=by_four(out_0[rows, columns]), in_=result[block][:, :, columns])
+
+        def store_codes(block, columns):
             nc.sync.dma_start(
-                out=out_0[512 * G : 512 * G + 512, f0:f1].rearrange("(p t) f -> p t f", t=4), in_=r_t[G][:, :, f0:f1]
+                out=out_1[block].rearrange("p m t -> p (m t)").bitcast(I32)[:, columns],
+                in_=out_codes[block][:, columns].bitcast(I32),
             )
 
-        def sp(G, f0, f1):
-            nc.sync.dma_start(
-                out=out_1[G].rearrange("p m t -> p (m t)").bitcast(I32)[:, f0:f1], in_=o_codes[G][:, f0:f1].bitcast(I32)
-            )
+        def store_scales(block):
             for q in range(4):
                 nc.sync.dma_start(
-                    out=out_2[G, 4 * q : 4 * q + 4, f0:f1].bitcast(I32),
-                    in_=o_sc[G][32 * q : 32 * q + 4, f0:f1].bitcast(I32),
+                    out=out_2[block, 4 * q : 4 * q + 4, :].bitcast(I32),
+                    in_=out_planes[block][32 * q : 32 * q + 4, :].bitcast(I32),
                 )
 
-        fns = dict(rx=rx, tx=tx, cx=cx, qx=qx, s1=s1, ch=ch, qh=qh, rd=rd, td=td, cd=cd, qd=qd, mm=mm, ad=ad, si=si, zc=zc, qo=qo, so=so, sp=sp)
         with tc.manual_schedule():
-            for key in ORDER:
-                fns[key[0]](*key[1:])
+            transpose_cells(0)
+            empty_cells(SCALAR, 0, 1)
+            empty_cells(VECTOR, 0, 0)
+            quantize_cells(0)
+            transpose_cells(1)
+            empty_cells(SCALAR, 1, 1)
+            empty_cells(VECTOR, 1, 0)
+            project(0, range(0, 4))
+            empty_hidden(SCALAR, 0, 2)
+            quantize_cells(1)
+            empty_hidden(VECTOR, 0, 0)
+            empty_hidden(VECTOR, 0, 1)
+            empty_hidden(VECTOR, 0, 3)
+            transpose_cells(2)
+            empty_cells(SCALAR, 2, 0)
+            quantize_hidden(0)
+            project(1, range(0, 4))
+            empty_cells(SCALAR, 2, 1)
+            empty_hidden(SCALAR, 1, 0)
+            empty_hidden(SCALAR, 1, 1)
+            quantize_cells(2)
+            empty_hidden(VECTOR, 1, 3)
+            transpose_cells(3)
+            empty_hidden(SCALAR, 1, 2)
+            empty_cells(SCALAR, 3, 1)
+            empty_cells(VECTOR, 3, 0)
+            project(2, range(0, 4))
+            empty_hidden(SCALAR, 2, 0)
+            empty_hidden(SCALAR, 2, 1)
+            quantize_hidden(1)
+            arrange_words(VECTOR, 1, 0)
+            quantize_cells(3)
+
+            transpose_incidence(0, 0)
+            empty_hidden(SCALAR, 2, 2)
+            empty_hidden(SCALAR, 2, 3)
+            arrange_words(VECTOR, 1, 1)
+            project(3, range(0, 2))
+            empty_incidence(SCALAR, 0, 0, 1)
+            arrange_words(VECTOR, 2, 1)
+            transpose_incidence(0, 1)
+            empty_incidence(SCALAR, 0, 0, 0)
+            empty_hidden(SCALAR, 3, 0)
+            quantize_hidden(2)
+            empty_incidence(VECTOR, 0, 1, 0)
+            transpose_incidence(1, 0)
+            empty_incidence(SCALAR, 0, 1, 1)
+            empty_incidence(SCALAR, 1, 0, 0)
+            empty_hidden(VECTOR, 3, 1)
+            quantize_incidence(0, 0, 1024)
+            project(3, range(2, 4))
+            empty_incidence(SCALAR, 1, 0, 1)
+            empty_hidden(SCALAR, 3, 2)
+            arrange_words(VECTOR, 2, 0)
+            transpose_incidence(1, 1)
+            empty_hidden(SCALAR, 3, 3)
+            empty_incidence(VECTOR, 1, 1, 1)
+
+            multiply(0, ALL, range(0, 2))
+            empty_incidence(SCALAR, 1, 1, 0)
+            arrange_words(SCALAR, 3, 0)
+            arrange_words(VECTOR, 3, 1)
+            quantize_incidence(1, 0, 1024)
+            transpose_incidence(2, 0)
+            empty_incidence(SCALAR, 2, 0, 0)
+            multiply(0, ALL, range(2, 4))
+            empty_incidence(SCALAR, 2, 0, 1)
+            quantize_hidden(3)
+            transpose_incidence(2, 1)
+            empty_incidence(SCALAR, 2, 1, 0)
+            arrange_words(VECTOR, 4, 1)
+            multiply(1, ALL, range(0, 2))
+            empty_incidence(SCALAR, 2, 1, 1)
+            arrange_words(SCALAR, 4, 0)
+            add_x1(0, ALL, 0)
+            quantize_incidence(2, 0, 1024)
+            transpose_incidence(3, 0)
+            empty_incidence(SCALAR, 3, 0, 1)
+            multiply(1, ALL, range(2, 4))
+            empty_incidence(VECTOR, 3, 0, 0)
+            add_x1(0, ALL, 1)
+            transpose_incidence(3, 1)
+            empty_incidence(SCALAR, 3, 1, 0)
+            add_x1(0, ALL, 2)
+            empty_incidence(VECTOR, 3, 1, 1)
+            multiply(2, ALL, range(0, 2))
+            silu(0, ALL, 0)
+            add_x1(0, ALL, 3)
+            quantize_incidence(3, 0, 1024)
+            transpose_incidence(4, 0)
+            silu(0, ALL, 2)
+            multiply(2, ALL, range(2, 4))
+            interleave(SCALAR, 0, RIGHT)
+            empty_incidence(VECTOR, 4, 0, 0)
+            interleave(VECTOR, 0, LEFT)
+            store_result(0, LEFT)
+            transpose_incidence(4, 1)
+            empty_incidence(SCALAR, 4, 1, 0)
+            quantize_result(0, LEFT)
+            quantize_result(0, RIGHT)
+            multiply(3, ALL, range(0, 2))
+            empty_incidence(SCALAR, 4, 0, 1)
+            empty_incidence(SCALAR, 4, 1, 1)
+            add_x1(1, ALL, 0)
+            add_x1(1, ALL, 1)
+            store_codes(0, LEFT)
+            store_result(0, RIGHT)
+            store_codes(0, RIGHT)
+            store_scales(0)
+            transpose_incidence(5, 0)
+            empty_incidence(SCALAR, 5, 0, 0)
+            empty_incidence(SCALAR, 5, 0, 1)
+            quantize_incidence(4, 0, 1024)
+            multiply(3, ALL, range(2, 4))
+            silu(1, ALL, 0)
+            add_x1(1, ALL, 2)
+            add_x1(1, ALL, 3)
+            transpose_incidence(5, 1)
+            empty_incidence(SCALAR, 5, 1, 0)
+            quantize_incidence(5, 0, 512)
+
+            multiply(4, LEFT, range(0, 4))
+            empty_incidence(SCALAR, 5, 1, 1)
+            silu(1, ALL, 2)
+            quantize_incidence(5, 512, 1024)
+            multiply(4, RIGHT, range(0, 2))
+            multiply(5, LEFT, range(0, 2))
+            interleave(SCALAR, 1, LEFT)
+            add_x1(2, LEFT, 0)
+            store_result(1, LEFT)
+            multiply(4, RIGHT, range(2, 4))
+            add_x1(2, LEFT, 1)
+            multiply(5, LEFT, range(2, 4))
+            interleave(SCALAR, 1, RIGHT)
+            quantize_result(1, LEFT)
+            multiply(5, RIGHT, range(0, 4))
+            add_x1(2, LEFT, 2)
+            add_x1(2, LEFT, 3)
+            silu(2, LEFT, 0)
+            silu(2, LEFT, 2)
+            store_codes(1, LEFT)
+            store_result(1, RIGHT)
+            add_x1(2, RIGHT, 0)
+            quantize_result(1, RIGHT)
+            store_codes(1, RIGHT)
+            store_scales(1)
+            add_x1(2, RIGHT, 1)
+            silu(2, RIGHT, 0)
+            add_x1(2, RIGHT, 2)
+            add_x1(2, RIGHT, 3)
+            silu(2, RIGHT, 2)
+            interleave(VECTOR, 2, LEFT)
+            quantize_result(2, LEFT)
+            interleave(VECTOR, 2, RIGHT)
+            quantize_result(2, RIGHT)
+            store_result(2, LEFT)
+            store_codes(2, LEFT)
+            store_result(2, RIGHT)
+            store_codes(2, RIGHT)
+            store_scales(2)

from contextlib import ExitStack

import concourse.mybir as mybir
from concourse.masks import make_identity

F32 = mybir.dt.float32
BF16 = mybir.dt.bfloat16
U32 = mybir.dt.uint32
I32 = mybir.dt.int32
U8 = mybir.dt.uint8
FP8X4 = mybir.dt.float8_e4m3fn_x4
SILU = mybir.ActivationFunctionType.Silu
ADD = mybir.AluOpType.add

EDGES, CELLS, FEATURES, OUT = 1536, 1024, 512, 512
FLOPS = 2 * (2 * CELLS * FEATURES * OUT) + 2 * (2 * EDGES * CELLS * OUT)

P = 128
PACK = 4
K_PASS = P * PACK
HALF_PASS = K_PASS // 2

ALL, LEFT, RIGHT = slice(0, 512), slice(0, 256), slice(256, 512)

VECTOR, SCALAR = "vector", "scalar"

ARRANGED = (1, 2, 3, 4)

BUFFERS = {"grouped": 6, "sorted": 2, "inc_grouped": 3, "inc_codes": 3, "inc_plane": 3, "z": 2}


def tile_simplicialboundarycoboundarymessage_x2_kernel(
    tc, x0, x1, x2, inc_down, inc_up, w0_words, w0_scales, w2_words, w2_scales, out_0, out_1, out_2
):
    nc = tc.nc
    cells, incidences = (x0, x2), (inc_down, inc_up)
    weight_words, weight_scales = (w0_words, w2_words), (w0_scales, w2_scales)

    with ExitStack() as ctx:
        keep = ctx.enter_context(tc.tile_pool(name="keep", bufs=1))
        turn = ctx.enter_context(tc.tile_pool(name="turn", bufs=1))
        psum = ctx.enter_context(tc.psum_pool(name="psum", bufs=1))

        def fixed(name, shape, dtype):
            return keep.tile(shape, dtype, name=name, tag=name, align_bytes=256)

        def shared(name, tag, shape, dtype):
            return turn.tile(shape, dtype, name=name, tag=tag, bufs=BUFFERS[tag], align_bytes=256)

        def bank(number, name, shape):
            return psum.tile(shape, F32, name=name, tag="bank%d" % number)

        zero = fixed("zero", [P, 1], F32)
        nc.vector.memset(zero[:], 0.0)
        identity = fixed("identity", [P, P], F32)
        make_identity(nc, identity[:])
        weight_codes, weight_planes = [], []
        for side in range(2):
            weight_codes.append(fixed("weight_codes%d" % side, [P, OUT], U32))
            plane = fixed("weight_plane%d" % side, [P, OUT], U8)
            nc.vector.memset(plane[:].bitcast(I32), 0)
            weight_planes.append(plane)
        nc.scalar.activation(out=zero[:], in_=zero[:], func=SILU)

        def by_four(rows):
            return rows.rearrange("(p t) c -> p t c", t=PACK)

        x_raw, inc_raw, x1_raw = {}, {}, {}

        def load_cells(i, slots=range(0, 4)):
            if i not in x_raw:
                x_raw[i] = fixed("x_raw%d" % i, [P, PACK, FEATURES], BF16)
            start = K_PASS * (i % 2)
            source = by_four(cells[i // 2][start : start + K_PASS, :])
            nc.sync.dma_start(out=x_raw[i][:, slots.start : slots.stop, :], in_=source[:, slots.start : slots.stop, :])

        def load_weight_scales(side):
            for q in range(4):
                nc.sync.dma_start(
                    out=weight_planes[side][32 * q : 32 * q + 4, :].bitcast(I32),
                    in_=weight_scales[side][0, 4 * q : 4 * q + 4, :].bitcast(I32),
                )

        def load_weight_words(side):
            nc.sync.dma_start(
                out=weight_codes[side][:].bitcast(I32),
                in_=weight_words[side][0].rearrange("p n t -> p (n t)").bitcast(I32),
            )

        def load_incidence(k):
            inc_raw[k] = fixed("inc_raw%d" % k, [P, PACK, CELLS], BF16)
            start = K_PASS * (k // 2)
            nc.sync.dma_start(out=inc_raw[k][:], in_=by_four(incidences[k % 2][start : start + K_PASS, :]))

        def load_x1(block):
            x1_raw[block] = fixed("x1_raw%d" % block, [P, PACK, OUT], BF16)
            nc.sync.dma_start(out=x1_raw[block][:], in_=by_four(x1[K_PASS * block : K_PASS * block + K_PASS, :]))

        load_cells(0, range(0, 2))
        load_cells(0, range(2, 4))
        load_cells(1)
        load_weight_scales(0)
        load_weight_words(0)
        load_cells(2)
        load_cells(3)
        load_weight_words(1)
        load_incidence(0)
        load_weight_scales(1)
        load_incidence(1)
        load_incidence(2)
        load_incidence(3)
        load_x1(0)
        load_incidence(4)
        load_incidence(5)
        load_x1(1)
        load_x1(2)

        def copy(engine, out, in_):
            if engine == VECTOR:
                nc.vector.tensor_copy(out=out, in_=in_)
            else:
                nc.scalar.copy(out=out, in_=in_)

        def quantize(codes, scales, grouped):
            nc.vector.quantize_mx(
                out=codes.bitcast(FP8X4), scales=scales, in_=grouped.rearrange("p c t -> p (c t)")
            )

        def as_words(tile):
            return tile[:].rearrange("p t k -> p (t k)").bitcast(F32)

        def transpose_pair(out, source_words, pair):
            for a in range(2):
                for u in range(2):
                    nc.tensor.transpose(out[:, 2 * a + u, :], source_words(2 * pair + a, u), identity[:])

        def empty_pair(engine, grouped, transposed, pair):
            words = grouped.rearrange("p c t -> p (c t)").bitcast(F32)[:, K_PASS * pair : K_PASS * pair + K_PASS]
            copy(
                engine,
                words.rearrange("p (a m u) -> p a m u", a=2, u=2),
                transposed[:].rearrange("p (a u) m -> p a m u", u=2),
            )

        x_banks = ((0, 1), (2, 3), (0, 1), (6, 7))
        h_banks = ((4, 5, 6, 7), (2, 3, 4, 5), (0, 1, 2, 3), (0, 1, 2, 3))
        x_turned, x_grouped, x_codes, x_planes = {}, {}, {}, {}
        h_sums, h_grouped, h_codes, h_planes = {}, {}, {}, {}

        def transpose_cells(i):
            words = as_words(x_raw[i])
            for pair in range(2):
                x_turned[i, pair] = bank(x_banks[i][pair], "x_turned%d%d" % (i, pair), [P, 4, P])

                def every_second_word(t, u):
                    first = HALF_PASS * t + u
                    return words[:, first : first + HALF_PASS - 1 : 2]

                transpose_pair(x_turned[i, pair], every_second_word, pair)

        def empty_cells(engine, i, pair):
            if i not in x_grouped:
                x_grouped[i] = shared("x_grouped%d" % i, "grouped", [P, K_PASS, PACK], BF16)
            empty_pair(engine, x_grouped[i][:], x_turned[i, pair], pair)

        def quantize_cells(i):
            x_codes[i] = fixed("x_codes%d" % i, [P, K_PASS], U32)
            x_planes[i] = fixed("x_plane%d" % i, [P, K_PASS], U8)
            quantize(x_codes[i][:], x_planes[i][:], x_grouped[i][:])

        def project(i, quarters):
            side = i // 2
            for j in quarters:
                h_sums[i, j] = bank(h_banks[i][j], "h_sums%d%d" % (i, j), [P, PACK, P])
                columns = slice(128 * j, 128 * j + 128)
                for t in range(4):
                    rows = slice(128 * t, 128 * t + 128)
                    nc.tensor.matmul_mx(
                        out=h_sums[i, j][:, t, :],
                        lhsT=x_codes[i][:, rows].bitcast(FP8X4),
                        lhsT_scale=x_planes[i][:, rows],
                        rhs=weight_codes[side][:, columns].bitcast(FP8X4),
                        rhs_scale=weight_planes[side][:, columns],
                        start=True,
                        stop=True,
                    )

        def empty_hidden(engine, i, j):
            if i not in h_grouped:
                h_grouped[i] = shared("h_grouped%d" % i, "grouped", [P, OUT, PACK], BF16)
            copy(engine, h_grouped[i][:, 128 * j : 128 * j + 128, :], h_sums[i, j][:].rearrange("p t n -> p n t"))

        def quantize_hidden(i):
            h_codes[i] = fixed("h_codes%d" % i, [P, OUT], U32)
            h_planes[i] = fixed("h_plane%d" % i, [P, OUT], U8)
            quantize(h_codes[i][:], h_planes[i][:], h_grouped[i][:])

        inc_sorted, inc_turned, inc_grouped, inc_codes, inc_planes, sums = {}, {}, {}, {}, {}, {}

        def arrange_words(engine, k, half):
            if k not in inc_sorted:
                inc_sorted[k] = shared("inc_sorted%d" % k, "sorted", [P, PACK, CELLS // 2], F32)
            source = as_words(inc_raw[k]).rearrange("p (s w u) -> p s u w", u=2, w=P)
            target = inc_sorted[k][:].rearrange("p t k -> p (t k)").rearrange("p (s u w) -> p s u w", u=2, w=P)
            runs = slice(4 * half, 4 * half + 4)
            copy(engine, target[:, runs], source[:, runs])

        def transpose_incidence(k, g):
            words = as_words(inc_raw[k])
            for pair in range(2):
                inc_turned[k, g, pair] = bank(4 + 2 * g + pair, "inc_turned%d%d%d" % (k, g, pair), [P, 4, P])

                def every_second_word(t, u):
                    first = (CELLS // 2) * t + HALF_PASS * g + u
                    return words[:, first : first + HALF_PASS - 1 : 2]

                def sorted_words(t, u):
                    first = HALF_PASS * g + P * u
                    return inc_sorted[k][:, t, first : first + P]

                transpose_pair(inc_turned[k, g, pair], sorted_words if k in ARRANGED else every_second_word, pair)

        def empty_incidence(engine, k, g, pair):
            if k not in inc_grouped:
                inc_grouped[k] = shared("inc_grouped%d" % k, "inc_grouped", [P, 2 * K_PASS, PACK], BF16)
            empty_pair(engine, inc_grouped[k][:, K_PASS * g : K_PASS * g + K_PASS, :], inc_turned[k, g, pair], pair)

        def quantize_incidence(k, first, end):
            if k not in inc_codes:
                inc_codes[k] = shared("inc_codes%d" % k, "inc_codes", [P, 2 * K_PASS], U32)
                inc_planes[k] = shared("inc_plane%d" % k, "inc_plane", [P, 2 * K_PASS], U8)
            columns = slice(first, end)
            quantize(inc_codes[k][:, columns], inc_planes[k][:, columns], inc_grouped[k][:, columns, :])

        def multiply(k, columns, slots):
            block, side = divmod(k, 2)
            for t in slots:
                key = (block, columns.start, t)
                if side == 0:
                    number = t + (4 if columns.start > 0 else 0)
                    sums[key] = bank(number, "sums%d_%d_%d" % key, [P, columns.stop - columns.start])
                for g in range(2):
                    rows = slice(K_PASS * g + 128 * t, K_PASS * g + 128 * t + 128)
                    nc.tensor.matmul_mx(
                        out=sums[key][:],
                        lhsT=inc_codes[k][:, rows].bitcast(FP8X4),
                        lhsT_scale=inc_planes[k][:, rows],
                        rhs=h_codes[2 * side + g][:, columns].bitcast(FP8X4),
                        rhs_scale=h_planes[2 * side + g][:, columns],
                        start=(side == 0 and g == 0),
                        stop=(side == 1 and g == 1),
                    )

        z, result, out_grouped, out_codes, out_planes = {}, {}, {}, {}, {}

        def add_x1(block, columns, t):
            if block not in z:
                z[block] = shared("z%d" % block, "z", [P, PACK, OUT], F32)
            nc.vector.tensor_tensor(
                out=z[block][:, t, columns],
                in0=sums[block, columns.start, t][:],
                in1=x1_raw[block][:, t, columns],
                op=ADD,
            )

        def silu(block, columns, t):
            if block not in result:
                result[block] = fixed("result%d" % block, [P, PACK, OUT], F32)
            nc.scalar.activation(
                out=result[block][:, t : t + 2, columns],
                in_=z[block][:, t : t + 2, columns],
                func=SILU,
                bias=zero[:],
            )

        def interleave(engine, block, columns):
            if block not in out_grouped:
                out_grouped[block] = shared("out_grouped%d" % block, "grouped", [P, OUT, PACK], BF16)
            copy(engine, out_grouped[block][:, columns, :], result[block][:, :, columns].rearrange("p t f -> p f t"))

        def quantize_result(block, columns):
            if block not in out_codes:
                out_codes[block] = fixed("out_codes%d" % block, [P, OUT], U32)
                out_planes[block] = fixed("out_plane%d" % block, [P, OUT], U8)
            quantize(out_codes[block][:, columns], out_planes[block][:, columns], out_grouped[block][:, columns, :])

        def store_result(block, columns):
            rows = slice(K_PASS * block, K_PASS * block + K_PASS)
            nc.sync.dma_start(out=by_four(out_0[rows, columns]), in_=result[block][:, :, columns])

        def store_codes(block, columns):
            nc.sync.dma_start(
                out=out_1[block].rearrange("p m t -> p (m t)").bitcast(I32)[:, columns],
                in_=out_codes[block][:, columns].bitcast(I32),
            )

        def store_scales(block):
            for q in range(4):
                nc.sync.dma_start(
                    out=out_2[block, 4 * q : 4 * q + 4, :].bitcast(I32),
                    in_=out_planes[block][32 * q : 32 * q + 4, :].bitcast(I32),
                )

        with tc.manual_schedule():
            transpose_cells(0)
            empty_cells(SCALAR, 0, 1)
            empty_cells(VECTOR, 0, 0)
            quantize_cells(0)
            transpose_cells(1)
            empty_cells(SCALAR, 1, 1)
            empty_cells(VECTOR, 1, 0)
            project(0, range(0, 4))
            empty_hidden(SCALAR, 0, 2)
            quantize_cells(1)
            empty_hidden(VECTOR, 0, 0)
            empty_hidden(VECTOR, 0, 1)
            empty_hidden(VECTOR, 0, 3)
            transpose_cells(2)
            empty_cells(SCALAR, 2, 0)
            quantize_hidden(0)
            project(1, range(0, 4))
            empty_cells(SCALAR, 2, 1)
            empty_hidden(SCALAR, 1, 0)
            empty_hidden(SCALAR, 1, 1)
            quantize_cells(2)
            empty_hidden(VECTOR, 1, 3)
            transpose_cells(3)
            empty_hidden(SCALAR, 1, 2)
            empty_cells(SCALAR, 3, 1)
            empty_cells(VECTOR, 3, 0)
            project(2, range(0, 4))
            empty_hidden(SCALAR, 2, 0)
            empty_hidden(SCALAR, 2, 1)
            quantize_hidden(1)
            arrange_words(VECTOR, 1, 0)
            quantize_cells(3)

            transpose_incidence(0, 0)
            empty_hidden(SCALAR, 2, 2)
            empty_hidden(SCALAR, 2, 3)
            arrange_words(VECTOR, 1, 1)
            project(3, range(0, 2))
            empty_incidence(SCALAR, 0, 0, 1)
            arrange_words(VECTOR, 2, 1)
            transpose_incidence(0, 1)
            empty_incidence(SCALAR, 0, 0, 0)
            empty_hidden(SCALAR, 3, 0)
            quantize_hidden(2)
            empty_incidence(VECTOR, 0, 1, 0)
            transpose_incidence(1, 0)
            empty_incidence(SCALAR, 0, 1, 1)
            empty_incidence(SCALAR, 1, 0, 0)
            empty_hidden(VECTOR, 3, 1)
            quantize_incidence(0, 0, 1024)
            project(3, range(2, 4))
            empty_incidence(SCALAR, 1, 0, 1)
            empty_hidden(SCALAR, 3, 2)
            arrange_words(VECTOR, 2, 0)
            transpose_incidence(1, 1)
            empty_hidden(SCALAR, 3, 3)
            empty_incidence(VECTOR, 1, 1, 1)

            multiply(0, ALL, range(0, 2))
            empty_incidence(SCALAR, 1, 1, 0)
            arrange_words(SCALAR, 3, 0)
            arrange_words(VECTOR, 3, 1)
            quantize_incidence(1, 0, 1024)
            transpose_incidence(2, 0)
            empty_incidence(SCALAR, 2, 0, 0)
            multiply(0, ALL, range(2, 4))
            empty_incidence(SCALAR, 2, 0, 1)
            quantize_hidden(3)
            transpose_incidence(2, 1)
            empty_incidence(SCALAR, 2, 1, 0)
            arrange_words(VECTOR, 4, 1)
            multiply(1, ALL, range(0, 2))
            empty_incidence(SCALAR, 2, 1, 1)
            arrange_words(SCALAR, 4, 0)
            add_x1(0, ALL, 0)
            quantize_incidence(2, 0, 1024)
            transpose_incidence(3, 0)
            empty_incidence(SCALAR, 3, 0, 1)
            multiply(1, ALL, range(2, 4))
            empty_incidence(VECTOR, 3, 0, 0)
            add_x1(0, ALL, 1)
            transpose_incidence(3, 1)
            empty_incidence(SCALAR, 3, 1, 0)
            add_x1(0, ALL, 2)
            empty_incidence(VECTOR, 3, 1, 1)
            multiply(2, ALL, range(0, 2))
            silu(0, ALL, 0)
            add_x1(0, ALL, 3)
            quantize_incidence(3, 0, 1024)
            transpose_incidence(4, 0)
            silu(0, ALL, 2)
            multiply(2, ALL, range(2, 4))
            interleave(SCALAR, 0, RIGHT)
            empty_incidence(VECTOR, 4, 0, 0)
            interleave(VECTOR, 0, LEFT)
            store_result(0, LEFT)
            transpose_incidence(4, 1)
            empty_incidence(SCALAR, 4, 1, 0)
            quantize_result(0, LEFT)
            quantize_result(0, RIGHT)
            multiply(3, ALL, range(0, 2))
            empty_incidence(SCALAR, 4, 0, 1)
            empty_incidence(SCALAR, 4, 1, 1)
            add_x1(1, ALL, 0)
            add_x1(1, ALL, 1)
            store_codes(0, LEFT)
            store_result(0, RIGHT)
            store_codes(0, RIGHT)
            store_scales(0)
            transpose_incidence(5, 0)
            empty_incidence(SCALAR, 5, 0, 0)
            empty_incidence(SCALAR, 5, 0, 1)
            quantize_incidence(4, 0, 1024)
            multiply(3, ALL, range(2, 4))
            silu(1, ALL, 0)
            add_x1(1, ALL, 2)
            add_x1(1, ALL, 3)
            transpose_incidence(5, 1)
            empty_incidence(SCALAR, 5, 1, 0)
            quantize_incidence(5, 0, 512)

            multiply(4, LEFT, range(0, 4))
            empty_incidence(SCALAR, 5, 1, 1)
            silu(1, ALL, 2)
            quantize_incidence(5, 512, 1024)
            multiply(4, RIGHT, range(0, 2))
            multiply(5, LEFT, range(0, 2))
            interleave(SCALAR, 1, LEFT)
            add_x1(2, LEFT, 0)
            store_result(1, LEFT)
            multiply(4, RIGHT, range(2, 4))
            add_x1(2, LEFT, 1)
            multiply(5, LEFT, range(2, 4))
            interleave(SCALAR, 1, RIGHT)
            quantize_result(1, LEFT)
            multiply(5, RIGHT, range(0, 4))
            add_x1(2, LEFT, 2)
            add_x1(2, LEFT, 3)
            silu(2, LEFT, 0)
            silu(2, LEFT, 2)
            store_codes(1, LEFT)
            store_result(1, RIGHT)
            add_x1(2, RIGHT, 0)
            quantize_result(1, RIGHT)
            store_codes(1, RIGHT)
            store_scales(1)
            add_x1(2, RIGHT, 1)
            silu(2, RIGHT, 0)
            add_x1(2, RIGHT, 2)
            add_x1(2, RIGHT, 3)
            silu(2, RIGHT, 2)
            interleave(VECTOR, 2, LEFT)
            quantize_result(2, LEFT)
            interleave(VECTOR, 2, RIGHT)
            quantize_result(2, RIGHT)
            store_result(2, LEFT)
            store_codes(2, LEFT)
            store_result(2, RIGHT)
            store_codes(2, RIGHT)
            store_scales(2)
